import numpy as np, ml_dtypes
CORES = [36,164,52,180,100,228,116,244]
N = 8
import mx_ref
BF = ml_dtypes.bfloat16
def gentries(a):
    return np.ascontiguousarray(a.reshape(8, 16, -1).transpose(0, 2, 1)).reshape(8, -1)
def gtable(e):
    e = np.asarray(e); return np.ascontiguousarray(e.reshape(8, -1, 16).transpose(0, 2, 1)).reshape(128, -1).astype(np.int32)
def gcols(t, e):
    v = np.concatenate([t.reshape(8, 16, -1, 4), np.zeros((8, 16, 1, 4), BF)], axis=2)
    return np.ascontiguousarray(np.stack([v[g][:, e[g]] for g in range(8)])).reshape(128, -1)
def gpick(z, e):
    return np.concatenate([z[16 * g:16 * g + 16][:, e[g]] for g in range(8)])
def tile(rs):
    return np.stack(rs, axis=2).reshape(128, -1).astype(BF)
def pick(q, e):
    c = np.concatenate([q[0].reshape(128, -1, 4), np.zeros((128, 1, 4), np.uint8)], axis=1); s = np.concatenate([q[1], np.ones((16, 1), np.uint8)], axis=1)
    return (np.ascontiguousarray(c[:, e].reshape(128, -1)), np.ascontiguousarray(s[:, e]))
def join(*qs):
    return (np.concatenate([q[0] for q in qs], axis=1), np.concatenate([q[1] for q in qs], axis=1))
def put(q, e, v):
    c, s = q[0].reshape(128, -1, 4).copy(), q[1].copy(); c[:, e] = v[0].reshape(128, -1, 4); s[:, e] = v[1]
    return (c.reshape(128, -1), s)
def pk(c, s):
    return (np.ascontiguousarray(c), mx_ref.live(s))
def emit(q):
    return q[0], q[1]
def packed(v, rng):
    q = [mx_ref.quantize(np.ascontiguousarray(v[r])) for r in range(N)]
    return np.stack([a for a, b in q]), np.stack([mx_ref.plane(b, rng) for a, b in q])
def values_of_codes():
    e, c = np.zeros((128, 128, 4), np.float32), np.zeros((128, 2, 4), np.uint8)
    e[np.arange(128), np.arange(128), 0] = 1
    c[:127, :, 0] = np.arange(256).reshape(2, 128).T[:127]
    return mx_ref.matmul(mx_ref.quantize(e.reshape(128, 512).astype(BF)), (c.reshape(128, 8), np.full((16, 2), 127, np.uint8))).T.reshape(-1).astype(np.float64)
CODE_VALUE, SCALE_VALUE = values_of_codes(), 2.0 ** (np.arange(256) - 127.0)
def decode(q):
    return (CODE_VALUE[q[0]].reshape(16, 8, -1, 4) * SCALE_VALUE[q[1]][:, None, :, None] + 0.0).reshape(128, -1).astype(np.float32)
def f(rng, *shape):
    return mx_ref.flush((rng.standard_normal(shape, dtype=np.float32) * np.exp2(rng.integers(-2, 3, shape[:-1] + (1,)))).astype(BF))
def wide(rng, *shape, cols=0):
    v = rng.standard_normal(shape, dtype=np.float32) * np.exp2(rng.integers(-12, 13, shape)).astype(np.float32)
    if cols: v *= np.repeat(np.exp2(rng.integers(-cols, cols + 1, shape[:-2] + (1, shape[-1] // 4))) * (rng.random(shape[:-2] + (1, shape[-1] // 4)) > 0.0625), 4, axis=-1).astype(np.float32)
    return mx_ref.flush(v.astype(BF))
C = 288
STEP = [1, 2, 4]
GROUP, PLACE = np.arange(8)[:, None], np.arange(C)
def numbers_of(rng):
    return {"x": np.array(f(rng, N, 128, 4 * C)), "u": np.array(f(rng, N, 128, 512)), "v": np.array(f(rng, N, 128, 512))}
def orders(rng):
    return rng.permuted(np.tile(np.arange(C), (N, 8, 1)), axis=2)
def paired(e):
    k = np.zeros_like(e)
    np.put_along_axis(k, e[:, :, 0::2], e[:, :, 1::2], 2)
    np.put_along_axis(k, e[:, :, 1::2], e[:, :, 0::2], 2)
    return k
def stored(p, q, mu):
    return {a: np.stack([gtable(k[r]) for r in range(N)]) for a, k in (("pl", p), ("ql", q), ("ml", mu))}
def lists(rng):
    return stored(paired(orders(rng)), paired(orders(rng)), paired(orders(rng)))
def layers(rng, still=[]):
    w = np.array(f(rng, N, 128, 2048)).reshape(N, 8, 16, 4, 8, 16, 4)
    for i in still:
        w[:, :, i] = 0
        w[:, :, :, :, :, i] = 0
    return w
def weights(rng, w):
    c, s = packed(np.ascontiguousarray(w).reshape(N, 128, 2048), rng)
    return {"wc": c, "ws": s}
def setup_inputs(rng):
    return {**numbers_of(rng), **lists(rng), **weights(rng, layers(rng))}
def setup_inputs_ties(rng):
    d = numbers_of(rng)
    e = orders(rng)
    mu = paired(orders(rng))
    k = np.zeros((N, 8, C))
    for r in range(N):
        h = rng.permutation(8)
        c = rng.integers(0, C, 2)
        k[r, h[1], min(c[0], mu[r, h[1], c[0]])] = -1
        k[r, h[2], max(c[1], mu[r, h[2], c[1]])] = -1
        k[r, h[3], e[r, h[3], :2]] = -1
        k[r, h[4]] = rng.integers(-4, 0, C)
        k[r, h[5]] = rng.integers(-1, 3, C)
        k[r, h[6]] = rng.integers(1, 4, C)
        k[r, h[7]] = rng.integers(0, 2, C)
        k[r, h[7], e[r, h[7], 0]] = -1
        k[r, h[7], e[r, h[7], 2 * rng.integers(1, C // 2)]] = -1
    x = d["x"].reshape(N, 8, 16, C, 4)
    x[:, :, 0] = 0
    x[:, :, 0, :, 0] = k.astype(np.float32).astype(BF)
    u = d["u"].reshape(N, 128, 128, 4)
    u[:, :, ::16] = 0
    for h in range(0, 128, 16): u[:, h, h, 0] = 1
    return {"x": x.reshape(N, 128, 4 * C), "u": u.reshape(N, 128, 512), "v": d["v"], **stored(paired(e), paired(np.roll(e, -1, axis=2)), mu), **weights(rng, layers(rng, [0]))}
def setup_inputs_near(rng):
    d = numbers_of(rng)
    x = d["x"].astype(np.float32).reshape(N, 8, 16, C, 4)
    x[:, :, :2] = 0
    x[:, :, 8:] = 0
    x[:, :, 1, :, 0] = rng.choice([-1.0, 1.0], (N, 8, C)) * (1.0 + 0.125 * rng.integers(0, 8, (N, 8, C))) * 2.0 ** -7
    u = d["u"].reshape(N, 128, 128, 4)
    u[:, :, ::16] = 0
    w = layers(rng, [0, 1, 8, 9, 10, 11, 12, 13, 14, 15])
    o = rng.permutation(N) % 4
    for r in range(N):
        c = rng.choice([-1.0, 1.0], (8, 1))
        s = rng.integers(0, 16, (8, C))
        digits = ((s[:, :, None] >> np.arange(4)) & 1) * np.exp2(np.arange(4) - 23.0)
        if o[r] < 2:
            x[r, :, 0, :, 0] = c
            x[r, :, 8] = digits
            x[r, :, 11, :, 0] = 2.0 ** -10
        elif o[r] == 2: x[r, :, 8] = digits * rng.choice([-1.0, 1.0], (8, C, 1))
        else:
            x[r, :, 8, :, 0] = np.where(s < 8, 1.25, 0.0) * 2.0 ** -29 * c
            x[r, :, 9, :, 0] = np.where(s < 8, 0.0, 1.125) * 2.0 ** -29 * c
            x[r, :, 12, :, 0] = 2.0 ** -28
            for g in range(8): w[r, g, 1, 0, g, 10, 0] = 2.0 ** -30
            for i, g in enumerate(rng.permutation(8)[:4]):
                if i < 2:
                    e = rng.choice([-1.0, 1.0], C) * 2.0 ** -29
                    x[r, g, 8, :, 0] = 1.25 * e
                    x[r, g, 9, :, 0] = -1.125 * e
                else:
                    x[r, g, 8:] = 0
                    x[r, g, 12, :, 0] = 2.0 ** -30
                    w[r, g, 1, 0, g, 10, 0] = -2.0 ** -30
                    w[r, g, 1, 0, g, 11, 0] = 2.0 ** -30
        at = [0, C - 1, int(rng.integers(C)), int(rng.integers(C))]
        for g, j in zip(rng.permutation(8)[:4], at): x[r, g, 0, j, 0] = 2.0 ** 29 * rng.choice([-1.0, 1.0])
        k = 1.0 if o[r] == 0 else 2.0 ** -30
        for h in range(0, 128, 16):
            u[r, h, h, 0] = k if o[r] < 2 else 1.0
            if o[r] < 2: u[r, h + 11, h, 0] = k
            if o[r] < 3: u[r, h + 8, h] = k
            else:
                u[r, h + 8, h, 0] = k
                u[r, h + 9, h, 0] = 1.125 * k
                u[r, h + 10, h, 0] = k
                u[r, h + 11, h, 0] = 1.125 * k
    return {"x": x.reshape(N, 128, 4 * C).astype(BF), "u": u.reshape(N, 128, 512), "v": d["v"], **lists(rng), **weights(rng, w)}
def setup_inputs_odd(rng):
    d = numbers_of(rng)
    x = (1.0 + (2 * rng.integers(0, 64, (N, 16, 8, C, 4)) + 1) * 2.0 ** -7) * np.exp2(-rng.integers(0, 7, (N, 16, 8, C, 4)).astype(np.float64)) * rng.choice([-1.0, 1.0], (N, 16, 8, C, 4))
    x[:, :, 0, :, 0] = 1.96875 * 2.0 ** 8 * rng.choice([-1.0, 1.0], (N, 16, C))
    x[:, 1::2, 0, :, 0] *= np.where(rng.random((N, 8, C)) < 0.5, 2.0 ** -6, 1.0)
    u = d["u"].reshape(N, 16, 8, 128, 4)
    u[:, :, 0, ::16] = 0
    for r in range(N):
        for i, g in enumerate(rng.permutation(8)[:4]):
            x[r, 2 * g, 1, :, 0] = (8 + rng.integers(0, 2, C)) * 2.0 ** (i - 8)
            u[r, :, :, 16 * g] = 0
            u[r, 2 * g, 1, 16 * g, 0] = 1.0
    return {"x": x.astype(np.float32).reshape(N, 128, 4 * C).astype(BF), "u": u.reshape(N, 128, 512), "v": d["v"], **lists(rng), **weights(rng, layers(rng, [0, 8]))}
def setup_inputs_ends(rng):
    d = numbers_of(rng)
    o, e = rng.permutation(N) % 2, rng.permutation(N) % 4
    sign = rng.choice([-1.0, 1.0], (128, 1, 4))
    half = np.repeat(rng.choice([0.5, 1.0], (N, 1, C, 2)), 2, axis=3)
    small = sign * (1.0 + 0.125 * rng.integers(0, 8, (N, 128, C, 4))) * 2.0 ** -30
    x = sign * half * (14 + rng.integers(0, 3, (N, 128, C, 4))) * 2.0 ** 26
    x[o == 1] = small[o == 1]
    x[:, 112:120] = sign[112:120]
    x[:, 120:] = small[:, 120:]
    size = np.where(o == 0, 2.0 ** 30, 2.0 ** -30)
    kinds = np.array([[1, 1, 1, 1]] * 2 + [[-1, -1, -1, -1]] * 3 + [[1, 1, -1, -1]] * 2 + [[0, 0, 0, 0]])
    u = d["u"].astype(np.float32).reshape(N, 128, 128, 4)
    for r in range(N): u[r, :, ::16] = sign * kinds[rng.permutation(8)][None] * size[r]
    u[:, 112:, ::16] = 0
    v = rng.choice([-1.0, 1.0], (N, 128, 512)) * size[:, None, None]
    a = orders(rng)
    p, q, mu = paired(a), paired(np.roll(a, -1, axis=2)), paired(orders(rng))
    q[e == 1] = p[e == 1]
    mu[e == 1] = p[e == 1]
    p[e == 2] = C - 1 - np.arange(C)
    q[e == 2] = np.arange(C) ^ 1
    q[e == 3] = paired(orders(rng))[e == 3]
    w = np.zeros((N, 128, 4, 128, 4), np.float32)
    i, n = np.arange(112), np.arange(8)
    for b in range(4):
        for r in range(N):
            if o[r] == 0: w[r, i, b, i, b] = -4.0
            w[r, (120 if b < 2 else 96) + n, b, 112 + n, b] = 2.0 ** 30 if b < 2 else 2.0 ** -30
    return {"x": x.astype(np.float32).reshape(N, 128, 4 * C).astype(BF), "u": u.reshape(N, 128, 512).astype(BF), "v": v.astype(np.float32).astype(BF), **stored(p, q, mu), **weights(rng, w.astype(BF))}
def setup_inputs_spread(rng):
    d = setup_inputs(rng)
    d["x"] = wide(rng, N, 128, 4 * C, cols=6)
    return d
def check_inputs(d):
    b = []
    for k in ("x", "u", "v"):
        a = np.abs(d[k].astype(np.float32))
        if not (np.isfinite(a).all() and ((a == 0) | (a >= 2.0 ** -30) & (a <= 2.0 ** 30)).all()): b.append("a value of " + k)
    for k in ("pl", "ql", "ml"):
        for r in range(N):
            e = gentries(d[k][r])
            if not ((e >= 0) & (e < C)).all(): b.append("an entry of " + k)
            elif (e == PLACE).any() or (e[GROUP, e] != PLACE).any(): b.append(k + ": no involution without fixed points")
    none, least, most = [emit(mx_ref.quantize(np.full((128, 16), k, np.float32).astype(BF)))[1][0, 0] for k in (0.0, 2.0 ** -30, 2.0 ** 30)]
    for r in range(N):
        if ((d["wc"][r] == 0x7F) | (d["wc"][r] == 0xFF)).any(): b.append("wc: a code that is no number")
        s = mx_ref.live(d["ws"][r])
        if ((s != none) & ((s < least) | (s > most))).any(): b.append("ws: a scale out of range")
        if (((d["wc"][r].reshape(16, 8, 512, 4) & 0x7F) != 0) & (s == none)[:, None, :, None]).any(): b.append("wc: a code other than zero under the scale of zeros")
    return b
def powers(a):
    k = [np.tile(PLACE, (8, 1))]
    for i in range(C // 2 - 1): k.append(a[GROUP, k[-1]])
    return np.stack(k)
def mirror(p, q, stop):
    ahead, back = powers(q[GROUP, p]), powers(p[GROUP, q])
    i, j = np.argmax(stop[GROUP, ahead], axis=0), np.argmax(stop[GROUP, back], axis=0)
    return ahead[i, GROUP, back[j, GROUP, PLACE]]
def reference(x, u, v, pl, ql, ml, wc, ws):
    qu = [mx_ref.quantize(u[r]) for r in range(N)]
    lay = [pk(wc[r], ws[r]) for r in range(N)]
    p, q, mu = [[gentries(a[r]).astype(np.int64) for r in range(N)] for a in (pl, ql, ml)]
    now = [x[r] for r in range(N)]
    for step in STEP:
        own, sent, image = [], [], []
        for r in range(N):
            t = mx_ref.quantize(now[r])
            s = mx_ref.matmul(qu[r], t)[::16] + np.float32(0.0)
            d = decode(t).astype(BF)
            m = mirror(p[r], q[r], s < 0)
            z = (gcols(d, m).astype(np.float32) + gcols(d, q[r][GROUP, p[r]]).astype(np.float32)) * np.float32(0.5)
            sent.append(mx_ref.quantize(z.astype(BF)))
            w = (PLACE < mu[r]) & (s[GROUP, m] > s[GROUP, m[GROUP, mu[r]]])
            e = np.where(w | w[GROUP, mu[r]], mu[r], PLACE)
            q[r] = e[GROUP, q[r][GROUP, e]]
            own.append(d)
            image.append(m)
        now = [tile([gpick(mx_ref.matmul(pick(lay[r], np.arange(128 * b, 128 * b + 128)), sent[r ^ step]) * np.float32(0.03125), image[r]) + own[r][:, b::4].astype(np.float32) for b in range(4)]) for r in range(N)]
    y, qo = np.zeros((N, 128, C), np.float32), np.zeros((N, 8, C), np.float32)
    oc, osc = np.zeros((N, 128, 4 * C), np.uint8), np.zeros((N, 16, C), np.uint8)
    for r in range(N):
        t = mx_ref.quantize(now[r])
        y[r] = mx_ref.matmul(mx_ref.quantize(v[r]), t)
        qo[r] = q[r]
        oc[r], osc[r] = emit(t)
    return {"y": y, "qo": qo, "oc": oc, "osc": osc}

@@ -1,0 +1,362 @@
+from concourse.bass import DstId, RemoteDMATransfer
+from concourse.mybir import dt, AluOpType as O, ActivationFunctionType as AF
+
+C = 288
+K = C // 16
+STEPS = [1, 2, 4]
+JUMPS = [(0, 1), (1, 2), (2, 4), (3, 8), (4, 16), (4, 16), (5, 32), (6, 64)]
+SEEN = 143
+MID = 144
+LIFT = 16
+HOLD, DROP = float(2 ** 19), float(-2 ** 21)
+GAIN = float(2 ** 20)
+
+F32, BF, F16, I32, U16, U8, MX = "float32", "bfloat16", "float16", "int32", "uint16", "uint8", "float8_e4m3fn_x4"
+
+
+def sb(n, d):
+    return ("sbuf", [128, n], d)
+
+
+SCRATCH = {
+    "xt": sb(4 * C, BF), "ut": sb(512, BF), "vt": sb(512, BF),
+    "pi": sb(K, I32), "qi": sb(K, I32), "mi": sb(K, I32),
+    "wq": sb(512, MX), "wp": sb(512, U8), "uq": sb(128, MX), "up": sb(128, U8), "ur": sb(128, MX), "urp": sb(128, U8),
+    "vq": sb(128, MX), "vp": sb(128, U8), "eq": sb(512, MX), "ep": sb(512, U8),
+    "tq": sb(C, MX), "tp": sb(C, U8), "zq": sb(C, MX), "zp": sb(C, U8),
+    "et": sb(2048, BF), "one": sb(512, BF), "zt": sb(4 * C, BF),
+    "cc": sb(2 * C, BF), "tm": sb(C, F32), "dif": sb(C, F32), "ka": sb(C, F32), "kb": sb(C, F32),
+    "hc": sb(C, F32), "hh": sb(2 * C, F16), "hm": sb(2 * C, BF), "ones": sb(2 * C, BF),
+    "onf": sb(C, F32),
+    "pp": sb(1, I32), "pm": sb(1, I32), "pf": sb(1, F32), "cor": sb(1, F32), "com": sb(1, F32), "coh": sb(1, F32),
+    "cw0": sb(K, F32), "cw": sb(K, F32), "ou0": sb(8, I32), "ou": sb(8, U16),
+    "w0": sb(C, F32), "wm0": sb(C, F32), "cd": sb(C, F32),
+    "pw": sb(K, U16), "qw": sb(K, U16), "muw": sb(K, U16), "dmw": sb(K, F32), "muf": sb(K, F32),
+    "qa": sb(C, BF), "qb": sb(C, BF), "ex": sb(C, F32), "eh": sb(2 * C, F16),
+    "wa": sb(C, F32), "wb": sb(C, F32), "wm": sb(C, F32),
+    "dd": sb(C, F32), "ctr": sb(C, F32), "c5": sb(C, F32), "buf": sb(C + 8, F32), "bg": sb(C, F32), "comb": sb(C, F32),
+    "vi": sb(K, I32), "li": sb(K, I32), "lw": sb(K, U16), "tw": sb(K, I32), "ci": sb(K, I32), "t2": sb(K, F32), "ll": sb(2 * K, I32),
+    "ps2": sb(2 * K, I32), "pos": sb(2 * K, U16), "posr": sb(K, U16), "lin": sb(2 * C, BF), "linw": sb(2 * K, U16),
+    "nf": sb(C, BF), "ss": sb(C, F32), "g2": sb(2 * C, BF), "fs": sb(2 * C, BF), "rs": sb(2 * C, BF), "ij": sb(2 * C, BF), "eij": sb(2 * C, BF),
+    "k2": sb(2 * K, F32), "k3": sb(2 * K, F32), "de": sb(K, F32), "zl": sb(K, F32), "zm": sb(K, F32), "dp": sb(K, F32), "of": sb(K, F32), "ow": sb(K, U16),
+    "mf": sb(C, BF), "mw": sb(K, U16),
+    "st": sb(C, F32), "su": sb(C, F32), "sd": sb(C, F32), "sg": sb(C, BF),
+    "sw": sb(K, U16), "sf": sb(C, BF), "yf": sb(C, BF), "yw": sb(K, U16),
+    "hb": sb(4 * C, BF), "ga": sb(4 * C, BF), "rb": sb(4 * C, F32), "mb": sb(4 * C, F32), "yo": sb(C, F32),
+    "ps": ("psum", [128, 4096], F32),
+}
+for _k in range(3):
+    SCRATCH["rq%d" % _k] = sb(C, MX)
+    SCRATCH["rp%d" % _k] = sb(C, U8)
+for _k in range(7):
+    SCRATCH["xf%d" % _k] = sb(C, BF)
+    SCRATCH["xw%d" % _k] = sb(K, U16)
+LOADS = ["pi", "qi", "mi", "xt", "ut", "vt", "wq", "wp"]
+STORES = ["oy", "oq", "occ", "oss"]
+SEMAPHORES = ["v", "s", "t", "g"] + ["ld_" + a for a in LOADS] + ["st_" + a for a in STORES] + ["arr%d" % k for k in range(3)] + ["snt%d" % k for k in range(3)]
+
+
+def rank_program(g, core, T, topo):
+    rank = T.rank_of(core)
+    if rank is None:
+        return
+    queue = {"v": g.vector, "s": g.scalar, "t": g.tensor, "g": g, "y": g.sync}
+    count, known, snap = {}, {e: {} for e in queue}, {}
+    last, readers = {}, {}
+
+    def settle(e, tokens):
+        for s, n in sorted(tokens, key=lambda a: (a[0] == e, -a[1])):
+            if known[e].get(s, 0) >= n: continue
+            queue[e].wait_ge(T.sem[s], n)
+            for a, b in list(snap.get((s, n), {}).items()) + [(s, n)]:
+                known[e][a] = max(known[e].get(a, 0), b)
+
+    def op(e, make, rd, wr, sem=None, inc=1):
+        tokens = set()
+        for k in rd:
+            if k in last: tokens.add(last[k])
+        for k in wr:
+            if k in last: tokens.add(last[k])
+            tokens |= readers.get(k, set())
+        settle(e, tokens)
+        ins, s = make(), sem or e
+        ins.then_inc(T.sem[s], inc)
+        count[s] = count.get(s, 0) + inc
+        token = (s, count[s])
+        snap[token] = dict(known[e])
+        snap[token][s] = count[s]
+        for k in wr: last[k], readers[k] = token, set()
+        for k in rd: readers.setdefault(k, set()).add(token)
+
+    V, S = g.vector, g.scalar
+
+    def ts(out, in0, s1, s2, o0, o1, rd, wr):
+        if o1 is None: op("v", lambda: V.tensor_scalar(out, in0, s1, None, o0), rd, wr)
+        else: op("v", lambda: V.tensor_scalar(out, in0, s1, s2, o0, o1), rd, wr)
+
+    def tt(out, a, b, o, rd, wr):
+        op("v", lambda: V.tensor_tensor(out, a, b, o), rd, wr)
+
+    def cp(out, a, rd, wr):
+        op("v", lambda: V.tensor_copy(out, a), rd, wr)
+
+    def act(out, a, f, rd, wr, bias=0.0, scale=1.0):
+        if bias == 0.0 and scale == 1.0: op("s", lambda: S.activation(out, a, f), rd, wr)
+        else: op("s", lambda: S.activation(out, a, f, bias=bias, scale=scale), rd, wr)
+
+    def scan(out, a, b, init, o0, o1, rd, wr):
+        op("v", lambda: V.tensor_tensor_scan(out, a, b, init, o0, o1), rd, wr)
+
+    def load(e, name, out, in_):
+        op(e, lambda: queue[e].dma_start(out, in_), [], [name], "ld_" + name, 16)
+
+    def held(name):
+        scan(T.ex[:], T.hc[:], T[name][:], 0.0, O.add, O.max, ["hc", name], ["ex"])
+        return T.ex[:, 15:C:16]
+
+    def unwrap(name, n, w):
+        scan(T.eh[:, 0:n], T.hh[:, 0:n], T[name][:, 0:n], 0.0, O.add, O.max, ["hh", name], ["eh"])
+        ts(T[w][:, 0:n // 16], T.eh[:, 15:n:16], T.coh[:, 0:1], None, O.subtract, None, ["eh", "coh"], [w])
+
+    def bank(b, n=C):
+        return T.ps[:, 512 * b:512 * b + n]
+
+    def mm(b, l, ls, a, r, rs):
+        op("t", lambda: g.tensor.matmul_mx(bank(b), T[l][:, a:a + 128], T[ls][:, a:a + 128], T[r][:, 0:C], T[rs][:, 0:C], True, True),
+           [l, ls, r, rs], ["ps%d" % b])
+
+    def quant(q, p, t, n, a=0):
+        op("v", lambda: V.quantize_mx(T[q][:, a:a + n], T[p][:, a:a + n], T[t][:, 4 * a:4 * a + 4 * n]), [t], [q, p])
+
+    def iota(name, out, pattern, base, mul, small=True):
+        if small: op("g", lambda: g.iota(out, pattern, base, mul, allow_small_or_imprecise_dtypes=True), [], [name])
+        else: op("g", lambda: g.iota(out, pattern, base, mul), [], [name])
+
+    load("y", "pi", T.pi[:], T.pl[:])
+    load("s", "qi", T.qi[:], T.ql[:])
+    load("y", "xt", T.xt[:], T.x[:])
+    load("y", "ut", T.ut[:], T.u[:])
+    load("y", "mi", T.mi[:], T.ml[:])
+    load("y", "wq", T.wq[:].bitcast(dt.uint8), T.wc[:])
+    load("y", "wp", T.wp[:], T.ws[:])
+    load("y", "vt", T.vt[:], T.v[:])
+
+    iota("pp", T.pp[:], [[1, 1]], 0, 1, False)
+    iota("tm", T.tm[:], [[0, K], [1, 16]], 0, 0)
+    iota("cc", T.cc[:, 0:C], [[1, C]], -MID, 0)
+    iota("wm0", T.wm0[:], [[256, C]], LIFT - 1, 0)
+    iota("w0", T.w0[:], [[256, C]], LIFT, 0)
+    iota("ou0", T.ou0[:], [[16, 8]], 0, 0, False)
+    iota("cw0", T.cw0[:], [[16, K]], 0, 0)
+    op("v", lambda: V.memset(T.one[:], 1.0), [], ["one"])
+    for b in range(4):
+        op("g", lambda: g.affine_select(T.et[:, 512 * b:512 * b + 512], T.one[:], [[-1, 512]], O.is_equal, 0.0, b, 4), ["one"], ["et%d" % b])
+    iota("cd", T.cd[:], [[256, C]], LIFT - 1 - SEEN, 0)
+    ts(T.pm[:], T.pp[:], 15, None, O.bitwise_and, None, ["pp"], ["pm"])
+    cp(T.pf[:], T.pm[:], ["pm"], ["pf"])
+    ts(T.cor[:], T.pf[:], 15.0, HOLD, O.is_lt, O.mult, ["pf"], ["cor"])
+    ts(T.dif[:], T.tm[:], T.pf[:, 0:1], None, O.subtract, None, ["tm", "pf"], ["dif"])
+    ts(T.ka[:], T.dif[:], 0.0, DROP, O.is_equal, O.mult, ["dif"], ["ka"])
+    ts(T.kb[:], T.dif[:], 1.0, HOLD, O.is_equal, O.mult, ["dif"], ["kb"])
+    tt(T.hc[:], T.ka[:], T.kb[:], O.add, ["ka", "kb"], ["hc"])
+    ts(T.hh[:, 0:C], T.hc[:], 2.0 ** -10, None, O.mult, None, ["hc"], ["hh"])
+    ts(T.coh[:], T.cor[:], 2.0 ** -10, float(MID), O.mult, O.subtract, ["cor"], ["coh"])
+
+    cp(T.qw[:], T.qi[:], ["qi"], ["qw"])
+    cp(T.pw[:], T.pi[:], ["pi"], ["pw"])
+    act(T.qa[:], T.cc[:, 0:C].indirect(T.qw[:]), AF.Copy, ["cc", "qw"], ["qa"])
+    act(T.xf0[:], T.qa[:].indirect(T.pw[:]), AF.Copy, ["qa", "pw"], ["xf0"])
+
+    def jump(hooks):
+        unwrap("xf0", C, "xw0")
+        w, wm, made = "w0", "wm0", 0
+        for n, (k, s) in enumerate(JUMPS):
+            if n:
+                act(T.wm[:], T[w][:], AF.Identity, [w], ["wm"], bias=-float(s))
+                wm = "wm"
+            if made == k and k < 6:
+                act(T["xf%d" % (k + 1)][:], T["xf%d" % k][:].indirect(T["xw%d" % k][:]), AF.Copy, ["xf%d" % k, "xw%d" % k], ["xf%d" % (k + 1)])
+            nxt = "wb" if w == "wa" else "wa"
+            tt(T[nxt][:], T[w][:].indirect(T["xw%d" % k][:]), T[wm][:], O.min, [w, "xw%d" % k, wm], [nxt])
+            w = nxt
+            if made == k and k < 6:
+                unwrap("xf%d" % (k + 1), C, "xw%d" % (k + 1))
+                made = k + 1
+            hooks.get(n, lambda: None)()
+        tt(T.dd[:], T[w][:].indirect(T.xw0[:]), T.cd[:], O.subtract, [w, "xw0", "cd"], ["dd"])
+        act(T.c5[:], T.dd[:], AF.Relu, ["dd"], ["c5"], scale=512.0)
+        act(T.ctr[:], T.dd[:], AF.Relu, ["dd"], ["ctr"])
+        a = held(w)
+        ts(T.li[:], a, T.cor[:, 0:1], 1.0 / 256, O.subtract, O.mult, ["ex", "cor"], ["li"])
+        ts(T.vi[:], a, T.cor[:, 0:1], float(SEEN - LIFT), O.subtract, O.add, ["ex", "cor"], ["vi"])
+        cp(T.lw[:], T.li[:], ["li"], ["lw"])
+        scan(T.buf[:, 1:C + 1], T.onf[:], T.c5[:], 0.0, O.mult, O.add, ["onf", "c5"], ["buf"])
+        act(T.bg[:], T.buf[:, 0:C].indirect(T.lw[:]), AF.Copy, ["buf", "lw"], ["bg"])
+        ts(T.tw[:], T.vi[:], 255, None, O.bitwise_and, None, ["vi"], ["tw"])
+        ts(T.t2[:], T.tw[:], 256.0, T.cor[:, 0:1], O.mult, O.subtract, ["tw", "cor"], ["t2"])
+        hooks.get(8, lambda: None)()
+        tt(T.comb[:], T.ctr[:].indirect(T.lw[:]), T.bg[:], O.add, ["ctr", "lw", "bg"], ["comb"])
+        a = held("comb")
+        tt(T.ci[:], a, T.t2[:], O.add, ["ex", "t2"], ["ci"])
+        ts(T.ps2[:, 0:K], T.ci[:], 8, None, O.arith_shift_right, None, ["ci"], ["psa"])
+        ts(T.ll[:, 0:K], T.ci[:], 255, None, O.bitwise_and, None, ["ci"], ["ll"])
+        tt(T.ps2[:, K:2 * K], T.ps2[:, 0:K], T.ll[:, 0:K], O.add, ["psa", "ll"], ["psb"])
+        cp(T.pos[:], T.ps2[:], ["psa", "psb"], ["pos"])
+        cp(T.lin[:].indirect(T.pos[:]), T.cc[:], ["pos", "cc"], ["lin"])
+        ts(T.ll[:, K:2 * K], T.ci[:], 255, None, O.bitwise_and, None, ["ci"], ["lm"])
+        ts(T.posr[:], T.ps2[:, 0:K], -1.0, float(2 * C - 1), O.mult, O.add, ["psa"], ["posr"])
+        hooks.get(9, lambda: None)()
+        unwrap("lin", 2 * C, "linw")
+        hooks.get(10, lambda: None)()
+
+    def products():
+        mm(4, "ur", "urp", 0, "tq", "tp")
+        for b in range(4): mm(b, "eq", "ep", 128 * b, "tq", "tp")
+
+    def halves(bs=range(4)):
+        for b in bs:
+            act(T.hb[:, C * b:C * b + C], bank(b), AF.Identity, [], ["ps%d" % b, "hb%d" % b], scale=0.5)
+
+    def aside():
+        for b in range(4):
+            act(T.ga[:, C * b:C * b + C], T.hb[:, C * b:C * b + C].indirect(T.xw0[:]), AF.Copy, ["hb%d" % b, "xw0"], ["ga%d" % b])
+
+    def prepare():
+        ts(T.ka[:], T.dif[:], 0.0, None, O.not_equal, None, ["dif"], ["ka"])
+        ts(T.kb[:], T.dif[:], 1.0, GAIN - 1.0, O.is_equal, O.mult, ["dif"], ["kb"])
+        tt(T.hm[:, 0:C], T.ka[:], T.kb[:], O.add, ["ka", "kb"], ["hm"])
+        cp(T.hm[:, C:2 * C], T.hm[:, 0:C], ["hm"], ["hm"])
+        cp(T.hh[:, C:2 * C], T.hh[:, 0:C], ["hh"], ["hh"])
+        cp(T.cc[:, C:2 * C], T.cc[:, 0:C], ["cc"], ["cc"])
+        ts(T.com[:], T.pf[:], 15.0, 1.0 / GAIN, O.is_ge, O.max, ["pf"], ["com"])
+        op("v", lambda: V.memset(T.ones[:], 1.0), [], ["ones"])
+        op("v", lambda: V.memset(T.onf[:], 1.0), [], ["onf"])
+        op("v", lambda: V.memset(T.buf[:], 0.0), [], ["buf"])
+
+    def prepare2():
+        ts(T.cw[:], T.cw0[:], T.pf[:, 0:1], None, O.add, None, ["cw0", "pf"], ["cw"])
+        cp(T.muw[:], T.mi[:], ["mi"], ["muw"])
+        cp(T.muf[:], T.mi[:], ["mi"], ["muf"])
+        tt(T.dmw[:], T.muf[:], T.cw[:], O.subtract, ["muf", "cw"], ["dmw"])
+
+    def first():
+        cp(T.ou[:], T.ou0[:], ["ou0"], ["ou"])
+        quant("uq", "up", "ut", 128)
+        cp(T.ur[:].bitcast(dt.uint32), T.uq[:].bitcast(dt.uint32).indirect(T.ou[:]), ["uq", "ou"], ["ur"])
+        cp(T.urp[:], T.up[:].indirect(T.ou[:]), ["up", "ou"], ["urp"])
+        quant("tq", "tp", "xt", C)
+
+    def constants():
+        for b in range(4):
+            op("v", lambda: V.quantize_mx(T.eq[:, 128 * b:128 * b + 128], T.ep[:, 128 * b:128 * b + 128], T.et[:, 512 * b:512 * b + 512]), ["et%d" % b], ["eq", "ep"])
+        products()
+
+    def lastly():
+        quant("vq", "vp", "vt", 128)
+        halves()
+        aside()
+
+    jump({0: prepare, 1: prepare2, 2: first, 3: constants, 8: lastly})
+
+    qcur = ["qa", "qb"]
+    for k, step in enumerate(STEPS):
+        final = k == 2
+        peer = T.cores[rank ^ step]
+        rid, pid = topo.addr(peer, core)
+        mask = topo.mask(core, peer)
+        width = len(topo.engines(core, peer))
+        ts(T.nf[:], bank(4), 0.0, None, O.is_ge, None, [], ["ps4", "nf"])
+        cp(T.g2[:, 0:C], T.nf[:].indirect(T.linw[:, 0:K]), ["nf", "linw"], ["g2a"])
+        act(T.g2[:, C:2 * C], T.nf[:].indirect(T.linw[:, K:2 * K]), AF.Copy, ["nf", "linw"], ["g2b"])
+        act(T.ss[:], bank(4), AF.Copy, [], ["ps4", "ss"])
+        scan(T.fs[:], T.g2[:], T.ones[:], 1.0, O.mult, O.add, ["g2a", "g2b", "ones"], ["fs"])
+        act(T.ij[:, 0:C], T.fs[:].indirect(T.pos[:, K:2 * K]), AF.Copy, ["fs", "pos"], ["ija"])
+        scan(T.rs[:], T.g2[:, ::-1], T.ones[:], 1.0, O.mult, O.add, ["g2a", "g2b", "ones"], ["rs"])
+        cp(T.ij[:, C:2 * C], T.rs[:].indirect(T.posr[:]), ["rs", "posr"], ["ijb"])
+        if k:
+            halves()
+            aside()
+        scan(T.eij[:], T.hm[:], T.ij[:], 1.0, O.mult, O.max, ["hm", "ija", "ijb"], ["eij"])
+        ts(T.k2[:], T.eij[:, 15:2 * C:16], T.com[:, 0:1], None, O.mult, None, ["eij", "com"], ["k2"])
+        tt(T.k3[:], T.k2[:], T.ll[:], O.min, ["k2", "ll", "lm"], ["k3"])
+        tt(T.de[:], T.k3[:, K:2 * K], T.k3[:, 0:K], O.subtract, ["k3"], ["de"])
+        ts(T.zl[:], T.de[:], 0.0, None, O.is_lt, None, ["de"], ["zl"])
+        tt(T.dp[:], T.de[:], T.ps2[:, 0:K], O.add, ["de", "psa"], ["dp"])
+        tt(T.zm[:], T.zl[:], T.ll[:, 0:K], O.mult, ["zl", "ll"], ["zm"])
+        tt(T.of[:], T.zm[:], T.dp[:], O.add, ["zm", "dp"], ["of"])
+        cp(T.ow[:], T.of[:], ["of"], ["ow"])
+        cp(T.mf[:], T.lin[:].indirect(T.ow[:]), ["lin", "ow"], ["mf"])
+        unwrap("mf", C, "mw")
+        for b in range(4):
+            tt(T.zt[:, b:4 * C:4], T.hb[:, C * b:C * b + C].indirect(T.mw[:]), T.ga[:, C * b:C * b + C], O.add, ["hb%d" % b, "mw", "ga%d" % b], ["zt"])
+            if b == 0:
+                act(T.st[:], T.ss[:].indirect(T.mw[:]), AF.Copy, ["ss", "mw"], ["st"])
+                act(T.su[:], T.st[:], AF.Copy, ["st"], ["su"])
+        quant("zq", "zp", "zt", C)
+        settle("g", {last["zq"], last["zp"]})
+        land, sent = T.sem["arr%d" % k], T.sem["snt%d" % k]
+        g.remote_dma(T["rq%d" % k][:].bitcast(dt.uint8), T.zq[:].bitcast(dt.uint8), land, sent, pid, rid, mask)
+        g.remote_dma(T["rp%d" % k][:], T.zp[:], land, sent, pid, rid, mask)
+        for a in ("zq", "zp"): readers.setdefault(a, set()).add(("snt%d" % k, 2 * width))
+        for a in ("rq%d" % k, "rp%d" % k): last[a] = ("arr%d" % k, 2 * width)
+        count["arr%d" % k] = count["snt%d" % k] = 2 * width
+        tt(T.sd[:], T.st[:].indirect(T.muw[:]), T.su[:], O.subtract, ["st", "muw", "su"], ["sd"])
+        act(T.sg[:], T.sd[:], AF.Sign, ["sd"], ["sg"])
+        scan(T.eh[:, 0:C], T.hh[:, 0:C], T.sg[:], 0.0, O.add, O.max, ["hh", "sg"], ["eh"])
+        ts(T.de[:], T.eh[:, 15:C:16], T.coh[:, 0:1], float(MID), O.subtract, O.subtract, ["eh", "coh"], ["de"])
+        tt(T.dp[:], T.de[:], T.dmw[:], O.mult, ["de", "dmw"], ["dp"])
+        ts(T.zl[:], T.dp[:], 0.0, None, O.is_lt, None, ["dp"], ["zl"])
+        tt(T.zm[:], T.zl[:], T.dmw[:], O.mult, ["zl", "dmw"], ["zm"])
+        tt(T.of[:], T.zm[:], T.cw[:], O.add, ["zm", "cw"], ["of"])
+        cp(T.sw[:], T.of[:], ["of"], ["sw"])
+        qo, qn = qcur[k % 2], qcur[1 - k % 2]
+        cp(T.yf[:], T[qo][:].indirect(T.sw[:]), [qo, "sw"], ["yf"])
+        act(T.sf[:], T.cc[:, 0:C].indirect(T.sw[:]), AF.Copy, ["cc", "sw"], ["sf"])
+        unwrap("yf", C, "yw")
+        cp(T[qn][:], T.sf[:].indirect(T.yw[:]), ["sf", "yw"], [qn])
+        if not final:
+            cp(T.xf0[:], T[qn][:].indirect(T.pw[:]), [qn, "pw"], ["xf0"])
+        else:
+            ts(T.dd[:], T[qn][:], float(MID), None, O.add, None, [qn], ["dd"])
+            op("y", lambda: g.sync.dma_start(T.qo[:], T.dd[0:128:16, :]), ["dd"], [], "st_oq", 16)
+
+        def layer():
+            for b in range(4): mm((5, 6, 7, 4)[b], "wq", "wp", 128 * b, "rq%d" % k, "rp%d" % k)
+
+        def scaled(bs):
+            for b in bs:
+                act(T.rb[:, C * b:C * b + C], bank((5, 6, 7, 4)[b]), AF.Identity, [], ["ps%d" % (5, 6, 7, 4)[b], "rb%d" % b], scale=0.03125)
+
+        def picked(bs):
+            for b in bs:
+                act(T.mb[:, C * b:C * b + C], T.rb[:, C * b:C * b + C].indirect(T.mw[:]), AF.Copy, ["rb%d" % b, "mw"], ["mb%d" % b])
+
+        def added(bs=range(4)):
+            for b in bs:
+                tt(T.xt[:, b:4 * C:4], T.mb[:, C * b:C * b + C], bank(b), O.add, ["mb%d" % b], ["ps%d" % b, "xt"])
+            quant("tq", "tp", "xt", C)
+
+        if not final:
+            def after_scatter():
+                added()
+                products()
+            jump({0: layer, 5: lambda: scaled([0]), 6: lambda: scaled([1]), 7: lambda: scaled([2]),
+                  8: lambda: (scaled([3]), picked(range(4))), 9: after_scatter})
+        else:
+            layer()
+            for b in (0, 1):
+                cp(T.ga[:, C * b:C * b + C], bank(b), [], ["ps%d" % b, "ga%d" % b])
+            for b, n in ((0, 5), (1, 6)):
+                ts(T.rb[:, C * b:C * b + C], bank(n), 0.03125, None, O.mult, None, [], ["ps%d" % n, "rb%d" % b])
+            scaled([2, 3])
+            picked([2, 3])
+            for b in (0, 1):
+                tt(T.xt[:, b:4 * C:4], T.rb[:, C * b:C * b + C].indirect(T.mw[:]), T.ga[:, C * b:C * b + C], O.add, ["rb%d" % b, "mw", "ga%d" % b], ["xt"])
+            added([2, 3])
+            op("y", lambda: g.sync.dma_start(T.oc[:], T.tq[:].bitcast(dt.uint8)), ["tq"], [], "st_occ", 16)
+            for a in range(4):
+                op("y", lambda: g.sync.dma_start(T.osc[4 * a:4 * a + 4, :], T.tp[32 * a:32 * a + 4, :]), ["tp"], [], "st_oss", 16)
+            mm(4, "vq", "vp", 0, "tq", "tp")
+            act(T.yo[:], bank(4), AF.Copy, [], ["ps4", "yo"])
+            op("y", lambda: g.sync.dma_start(T.y[:], T.yo[:]), ["yo"], [], "st_oy", 16)
+    settle("g", set(count.items()))

@@ -6,8 +6,10 @@ K = C // 16
 STEPS = [1, 2, 4]
 JUMPS = [(0, 1), (1, 2), (2, 4), (3, 8), (4, 16), (4, 16), (5, 32), (6, 64)]
 SEEN = 143
+CUT = 20
+TINY, PLAIN, HALF, GATHER, SCATTER, NEAR, WAKE, BIAS, LOOK, SLACK, FLIGHT = 0.09, 0.31, 0.17, 0.52, 2.2, 0.08, 0.16, 0.5, 0.5, 0.1, 6.0
 MID = 144
-LIFT = 16
+UNIT, LIFT = 512, 8
 HOLD, DROP = float(2 ** 19), float(-2 ** 21)
 GAIN = float(2 ** 20)
 
@@ -31,7 +33,7 @@ SCRATCH = {
     "pp": sb(1, I32), "pm": sb(1, I32), "pf": sb(1, F32), "cor": sb(1, F32), "com": sb(1, F32), "coh": sb(1, F32),
     "cw0": sb(K, F32), "cw": sb(K, F32), "ou0": sb(8, I32), "ou": sb(8, U16),
     "w0": sb(C, F32), "wm0": sb(C, F32), "cd": sb(C, F32),
-    "pw": sb(K, U16), "qw": sb(K, U16), "muw": sb(K, U16), "dmw": sb(K, F32), "muf": sb(K, F32),
+    "pw": sb(K, U16), "qw": sb(K, U16), "low": sb(K, U16), "hiw": sb(K, U16), "dmw": sb(K, F32), "muf": sb(K, F32),
     "qa": sb(C, BF), "qb": sb(C, BF), "ex": sb(C, F32), "eh": sb(2 * C, F16),
     "wa": sb(C, F32), "wb": sb(C, F32), "wm": sb(C, F32),
     "dd": sb(C, F32), "ctr": sb(C, F32), "c5": sb(C, F32), "buf": sb(C + 8, F32), "bg": sb(C, F32), "comb": sb(C, F32),
@@ -40,7 +42,7 @@ SCRATCH = {
     "nf": sb(C, BF), "ss": sb(C, F32), "g2": sb(2 * C, BF), "fs": sb(2 * C, BF), "rs": sb(2 * C, BF), "ij": sb(2 * C, BF), "eij": sb(2 * C, BF),
     "k2": sb(2 * K, F32), "k3": sb(2 * K, F32), "de": sb(K, F32), "zl": sb(K, F32), "zm": sb(K, F32), "dp": sb(K, F32), "of": sb(K, F32), "ow": sb(K, U16),
     "mf": sb(C, BF), "mw": sb(K, U16),
-    "st": sb(C, F32), "su": sb(C, F32), "sd": sb(C, F32), "sg": sb(C, BF),
+    "st": sb(C, F32), "su": sb(C, F32), "sg": sb(C, BF),
     "sw": sb(K, U16), "sf": sb(C, BF), "yf": sb(C, BF), "yw": sb(K, U16),
     "hb": sb(4 * C, BF), "ga": sb(4 * C, BF), "rb": sb(4 * C, F32), "mb": sb(4 * C, F32), "yo": sb(C, F32),
     "ps": ("psum", [128, 4096], F32),
@@ -71,66 +73,119 @@ def rank_program(g, core, T, topo):
             for a, b in list(snap.get((s, n), {}).items()) + [(s, n)]:
                 known[e][a] = max(known[e].get(a, 0), b)
 
-    def op(e, make, rd, wr, sem=None, inc=1):
+    def issue(n, e):
         tokens = set()
-        for k in rd:
+        for k in n["rd"]:
             if k in last: tokens.add(last[k])
-        for k in wr:
+        for k in n["wr"]:
             if k in last: tokens.add(last[k])
             tokens |= readers.get(k, set())
         settle(e, tokens)
-        ins, s = make(), sem or e
-        ins.then_inc(T.sem[s], inc)
-        count[s] = count.get(s, 0) + inc
+        s = n["sem"] or e
+        n["make"][e]().then_inc(T.sem[s], n["inc"])
+        count[s] = count.get(s, 0) + n["inc"]
         token = (s, count[s])
         snap[token] = dict(known[e])
         snap[token][s] = count[s]
-        for k in wr: last[k], readers[k] = token, set()
-        for k in rd: readers.setdefault(k, set()).add(token)
+        for k in n["wr"]: last[k], readers[k] = token, set()
+        for k in n["rd"]: readers.setdefault(k, set()).add(token)
+
+    nodes = []
+
+    def op(e, make, rd, wr, sem=None, inc=1, cost=TINY, lat=0.0, other=None, send=None):
+        nodes.append(dict(make={e: make} if other is None else {e: make, other[0]: other[1]}, rd=rd, wr=wr, sem=sem, inc=inc, cost=cost, lat=lat, send=send))
 
     V, S = g.vector, g.scalar
 
-    def ts(out, in0, s1, s2, o0, o1, rd, wr):
-        if o1 is None: op("v", lambda: V.tensor_scalar(out, in0, s1, None, o0), rd, wr)
-        else: op("v", lambda: V.tensor_scalar(out, in0, s1, s2, o0, o1), rd, wr)
+    def ts(out, in0, s1, s2, o0, o1, rd, wr, cost=TINY):
+        if o1 is None: op("v", lambda: V.tensor_scalar(out, in0, s1, None, o0), rd, wr, cost=cost)
+        else: op("v", lambda: V.tensor_scalar(out, in0, s1, s2, o0, o1), rd, wr, cost=cost)
 
-    def tt(out, a, b, o, rd, wr):
-        op("v", lambda: V.tensor_tensor(out, a, b, o), rd, wr)
+    def tt(out, a, b, o, rd, wr, cost=TINY):
+        op("v", lambda: V.tensor_tensor(out, a, b, o), rd, wr, cost=cost)
 
-    def cp(out, a, rd, wr):
-        op("v", lambda: V.tensor_copy(out, a), rd, wr)
+    def cp(out, a, rd, wr, cost=TINY):
+        op("v", lambda: V.tensor_copy(out, a), rd, wr, cost=cost)
 
-    def act(out, a, f, rd, wr, bias=0.0, scale=1.0):
-        if bias == 0.0 and scale == 1.0: op("s", lambda: S.activation(out, a, f), rd, wr)
-        else: op("s", lambda: S.activation(out, a, f, bias=bias, scale=scale), rd, wr)
+    def either(out, a, rd, wr, cost=GATHER):
+        op("s", lambda: S.activation(out, a, AF.Copy), rd, wr, cost=cost, other=("v", lambda: V.tensor_copy(out, a)))
 
-    def scan(out, a, b, init, o0, o1, rd, wr):
-        op("v", lambda: V.tensor_tensor_scan(out, a, b, init, o0, o1), rd, wr)
+    def act(out, a, f, rd, wr, bias=0.0, scale=1.0, cost=GATHER):
+        if bias == 0.0 and scale == 1.0: op("s", lambda: S.activation(out, a, f), rd, wr, cost=cost)
+        else: op("s", lambda: S.activation(out, a, f, bias=bias, scale=scale), rd, wr, cost=PLAIN)
+
+    def scan(out, a, b, init, o0, o1, rd, wr, cost=PLAIN):
+        op("v", lambda: V.tensor_tensor_scan(out, a, b, init, o0, o1), rd, wr, cost=cost)
 
     def load(e, name, out, in_):
-        op(e, lambda: queue[e].dma_start(out, in_), [], [name], "ld_" + name, 16)
+        op(e, lambda: queue[e].dma_start(out, in_), [], [name], "ld_" + name, 16, cost=0.1, lat=2.5)
+
+    def ordered():
+        wrote, read, preds, succ = {}, {}, [], []
+        for i, n in enumerate(nodes):
+            p = set()
+            for k in n["rd"]:
+                if k in wrote: p.add(wrote[k])
+            for k in n["wr"]:
+                if k in wrote: p.add(wrote[k])
+                p |= read.get(k, set())
+            for k in n["wr"]: wrote[k], read[k] = i, set()
+            for k in n["rd"]: read.setdefault(k, set()).add(i)
+            p.discard(i)
+            preds.append(p)
+            succ.append([])
+            for j in p: succ[j].append(i)
+        rank_ = [0.0] * len(nodes)
+        for i in range(len(nodes) - 1, -1, -1):
+            rank_[i] = nodes[i]["cost"] + nodes[i]["lat"] + max([rank_[j] + WAKE for j in succ[i]] + [0.0])
+        free, at, end, todo = {e: 0.0 for e in queue}, {}, {}, [len(p) for p in preds]
+        open_, out = [i for i in range(len(nodes)) if not preds[i]], []
+        while open_:
+            best, spots = {}, {}
+            waiting = min([max([end[j] + (NEAR if at[j] == "v" else WAKE) for j in preds[i]] + [0.0]) for i in open_ if list(nodes[i]["make"]) == ["v"]] + [1e9])
+            for i in open_:
+                spot = None
+                for e in nodes[i]["make"]:
+                    r = max([end[j] + (NEAR if at[j] == e else WAKE) for j in preds[i]] + [0.0])
+                    t = max(r, free[e])
+                    a = (t + (BIAS if e == "v" and len(nodes[i]["make"]) > 1 and waiting < t + GATHER * LOOK else 0.0), e, r)
+                    if spot is None or a < spot: spot = a
+                spots[i] = spot
+                e, r = spot[1], max(spot[2], free[spot[1]])
+                best[e] = min(best.get(e, 1e9), r)
+            e = min(best, key=lambda a: (best[a], a))
+            i = max([j for j in open_ if spots[j][1] == e and max(spots[j][2], free[e]) <= best[e] + SLACK], key=lambda j: (rank_[j], -j))
+            t = max(spots[i][2], free[e])
+            free[e], at[i], end[i] = t + nodes[i]["cost"], e, t + nodes[i]["cost"] + nodes[i]["lat"]
+            open_.remove(i)
+            out.append((nodes[i], e))
+            for j in succ[i]:
+                todo[j] -= 1
+                if not todo[j]: open_.append(j)
+        return out
 
     def held(name):
         scan(T.ex[:], T.hc[:], T[name][:], 0.0, O.add, O.max, ["hc", name], ["ex"])
         return T.ex[:, 15:C:16]
 
-    def unwrap(name, n, w):
-        scan(T.eh[:, 0:n], T.hh[:, 0:n], T[name][:, 0:n], 0.0, O.add, O.max, ["hh", name], ["eh"])
+    def unwrap(name, n, w, more=[]):
+        scan(T.eh[:, 0:n], T.hh[:, 0:n], T[name][:, 0:n], 0.0, O.add, O.max, ["hh", name] + more, ["eh"], HALF * n / C)
         ts(T[w][:, 0:n // 16], T.eh[:, 15:n:16], T.coh[:, 0:1], None, O.subtract, None, ["eh", "coh"], [w])
 
     def bank(b, n=C):
         return T.ps[:, 512 * b:512 * b + n]
 
-    def mm(b, l, ls, a, r, rs):
+    def mm(b, l, ls, a, r, rs, key=None):
         op("t", lambda: g.tensor.matmul_mx(bank(b), T[l][:, a:a + 128], T[ls][:, a:a + 128], T[r][:, 0:C], T[rs][:, 0:C], True, True),
-           [l, ls, r, rs], ["ps%d" % b])
+           [r, rs] + ([key] if key else [l, ls]), ["ps%d" % b], cost=0.3)
 
-    def quant(q, p, t, n, a=0):
-        op("v", lambda: V.quantize_mx(T[q][:, a:a + n], T[p][:, a:a + n], T[t][:, 4 * a:4 * a + 4 * n]), [t], [q, p])
+    def quant(q, p, t, n, rd=None):
+        op("v", lambda: V.quantize_mx(T[q][:, 0:n], T[p][:, 0:n], T[t][:, 0:4 * n]), rd or [t], [q, p], cost=0.32)
 
     def iota(name, out, pattern, base, mul, small=True):
-        if small: op("g", lambda: g.iota(out, pattern, base, mul, allow_small_or_imprecise_dtypes=True), [], [name])
-        else: op("g", lambda: g.iota(out, pattern, base, mul), [], [name])
+        cost = 0.14 + 0.002 * (C if len(pattern) > 1 else pattern[0][1])
+        if small: op("g", lambda: g.iota(out, pattern, base, mul, allow_small_or_imprecise_dtypes=True), [], [name], cost=cost)
+        else: op("g", lambda: g.iota(out, pattern, base, mul), [], [name], cost=cost)
 
     load("y", "pi", T.pi[:], T.pl[:])
     load("s", "qi", T.qi[:], T.ql[:])
@@ -144,14 +199,14 @@ def rank_program(g, core, T, topo):
     iota("pp", T.pp[:], [[1, 1]], 0, 1, False)
     iota("tm", T.tm[:], [[0, K], [1, 16]], 0, 0)
     iota("cc", T.cc[:, 0:C], [[1, C]], -MID, 0)
-    iota("wm0", T.wm0[:], [[256, C]], LIFT - 1, 0)
-    iota("w0", T.w0[:], [[256, C]], LIFT, 0)
+    iota("wm0", T.wm0[:], [[UNIT, C]], LIFT + SEEN - 1, 0)
+    iota("w0", T.w0[:], [[UNIT, C]], LIFT + SEEN, 0)
     iota("ou0", T.ou0[:], [[16, 8]], 0, 0, False)
     iota("cw0", T.cw0[:], [[16, K]], 0, 0)
     op("v", lambda: V.memset(T.one[:], 1.0), [], ["one"])
     for b in range(4):
-        op("g", lambda: g.affine_select(T.et[:, 512 * b:512 * b + 512], T.one[:], [[-1, 512]], O.is_equal, 0.0, b, 4), ["one"], ["et%d" % b])
-    iota("cd", T.cd[:], [[256, C]], LIFT - 1 - SEEN, 0)
+        op("g", lambda b=b: g.affine_select(T.et[:, 512 * b:512 * b + 512], T.one[:], [[-1, 512]], O.is_equal, 0.0, b, 4), ["one"], ["et%d" % b], cost=1.2)
+    iota("cd", T.cd[:], [[UNIT, C]], LIFT - 1, 0)
     ts(T.pm[:], T.pp[:], 15, None, O.bitwise_and, None, ["pp"], ["pm"])
     cp(T.pf[:], T.pm[:], ["pm"], ["pf"])
     ts(T.cor[:], T.pf[:], 15.0, HOLD, O.is_lt, O.mult, ["pf"], ["cor"])
@@ -166,81 +221,78 @@ def rank_program(g, core, T, topo):
     cp(T.pw[:], T.pi[:], ["pi"], ["pw"])
     act(T.qa[:], T.cc[:, 0:C].indirect(T.qw[:]), AF.Copy, ["cc", "qw"], ["qa"])
     act(T.xf0[:], T.qa[:].indirect(T.pw[:]), AF.Copy, ["qa", "pw"], ["xf0"])
+    op("v", lambda: V.memset(T.ones[:], 1.0), [], ["ones"], cost=PLAIN)
+    op("v", lambda: V.memset(T.onf[:], 1.0), [], ["onf"], cost=PLAIN)
+    op("v", lambda: V.memset(T.buf[:], 0.0), [], ["buf"], cost=PLAIN)
+    cp(T.cc[:, C:2 * C], T.cc[:, 0:C], ["cc"], ["cd2"], HALF)
+    cp(T.hh[:, C:2 * C], T.hh[:, 0:C], ["hh"], ["hh2"], HALF)
+    cp(T.ou[:], T.ou0[:], ["ou0"], ["ou"])
 
-    def jump(hooks):
+    def jump():
         unwrap("xf0", C, "xw0")
         w, wm, made = "w0", "wm0", 0
         for n, (k, s) in enumerate(JUMPS):
             if n:
                 act(T.wm[:], T[w][:], AF.Identity, [w], ["wm"], bias=-float(s))
                 wm = "wm"
-            if made == k and k < 6:
-                act(T["xf%d" % (k + 1)][:], T["xf%d" % k][:].indirect(T["xw%d" % k][:]), AF.Copy, ["xf%d" % k, "xw%d" % k], ["xf%d" % (k + 1)])
             nxt = "wb" if w == "wa" else "wa"
-            tt(T[nxt][:], T[w][:].indirect(T["xw%d" % k][:]), T[wm][:], O.min, [w, "xw%d" % k, wm], [nxt])
+            tt(T[nxt][:], T[w][:].indirect(T["xw%d" % k][:]), T[wm][:], O.min, [w, "xw%d" % k, wm], [nxt], GATHER)
             w = nxt
             if made == k and k < 6:
+                either(T["xf%d" % (k + 1)][:], T["xf%d" % k][:].indirect(T["xw%d" % k][:]), ["xf%d" % k, "xw%d" % k], ["xf%d" % (k + 1)])
                 unwrap("xf%d" % (k + 1), C, "xw%d" % (k + 1))
                 made = k + 1
-            hooks.get(n, lambda: None)()
-        tt(T.dd[:], T[w][:].indirect(T.xw0[:]), T.cd[:], O.subtract, [w, "xw0", "cd"], ["dd"])
+        tt(T.dd[:], T[w][:].indirect(T.xw0[:]), T.cd[:], O.subtract, [w, "xw0", "cd"], ["dd"], GATHER)
         act(T.c5[:], T.dd[:], AF.Relu, ["dd"], ["c5"], scale=512.0)
-        act(T.ctr[:], T.dd[:], AF.Relu, ["dd"], ["ctr"])
+        act(T.ctr[:], T.dd[:], AF.Relu, ["dd"], ["ctr"], cost=PLAIN)
         a = held(w)
-        ts(T.li[:], a, T.cor[:, 0:1], 1.0 / 256, O.subtract, O.mult, ["ex", "cor"], ["li"])
-        ts(T.vi[:], a, T.cor[:, 0:1], float(SEEN - LIFT), O.subtract, O.add, ["ex", "cor"], ["vi"])
-        cp(T.lw[:], T.li[:], ["li"], ["lw"])
+        ts(T.lw[:], a, T.cor[:, 0:1], 1.0 / UNIT, O.subtract, O.mult, ["ex", "cor"], ["lw"])
+        ts(T.vi[:], a, T.cor[:, 0:1], float(LIFT), O.subtract, O.subtract, ["ex", "cor"], ["vi"])
         scan(T.buf[:, 1:C + 1], T.onf[:], T.c5[:], 0.0, O.mult, O.add, ["onf", "c5"], ["buf"])
-        act(T.bg[:], T.buf[:, 0:C].indirect(T.lw[:]), AF.Copy, ["buf", "lw"], ["bg"])
-        ts(T.tw[:], T.vi[:], 255, None, O.bitwise_and, None, ["vi"], ["tw"])
+        either(T.bg[:], T.buf[:, 0:C].indirect(T.lw[:]), ["buf", "lw"], ["bg"])
+        ts(T.tw[:], T.vi[:], UNIT - 1, None, O.bitwise_and, None, ["vi"], ["tw"])
         ts(T.t2[:], T.tw[:], 256.0, T.cor[:, 0:1], O.mult, O.subtract, ["tw", "cor"], ["t2"])
-        hooks.get(8, lambda: None)()
-        tt(T.comb[:], T.ctr[:].indirect(T.lw[:]), T.bg[:], O.add, ["ctr", "lw", "bg"], ["comb"])
+        tt(T.comb[:], T.ctr[:].indirect(T.lw[:]), T.bg[:], O.add, ["ctr", "lw", "bg"], ["comb"], GATHER)
         a = held("comb")
         tt(T.ci[:], a, T.t2[:], O.add, ["ex", "t2"], ["ci"])
         ts(T.ps2[:, 0:K], T.ci[:], 8, None, O.arith_shift_right, None, ["ci"], ["psa"])
         ts(T.ll[:, 0:K], T.ci[:], 255, None, O.bitwise_and, None, ["ci"], ["ll"])
         tt(T.ps2[:, K:2 * K], T.ps2[:, 0:K], T.ll[:, 0:K], O.add, ["psa", "ll"], ["psb"])
         cp(T.pos[:], T.ps2[:], ["psa", "psb"], ["pos"])
-        cp(T.lin[:].indirect(T.pos[:]), T.cc[:], ["pos", "cc"], ["lin"])
+        cp(T.lin[:].indirect(T.pos[:]), T.cc[:], ["pos", "cc", "cd2"], ["lin"], SCATTER)
         ts(T.ll[:, K:2 * K], T.ci[:], 255, None, O.bitwise_and, None, ["ci"], ["lm"])
         ts(T.posr[:], T.ps2[:, 0:K], -1.0, float(2 * C - 1), O.mult, O.add, ["psa"], ["posr"])
-        hooks.get(9, lambda: None)()
-        unwrap("lin", 2 * C, "linw")
-        hooks.get(10, lambda: None)()
+        unwrap("lin", 2 * C, "linw", ["hh2"])
 
     def products():
         mm(4, "ur", "urp", 0, "tq", "tp")
-        for b in range(4): mm(b, "eq", "ep", 128 * b, "tq", "tp")
+        for b in range(4): mm(b, "eq", "ep", 128 * b, "tq", "tp", "eq%d" % b)
 
-    def halves(bs=range(4)):
-        for b in bs:
-            act(T.hb[:, C * b:C * b + C], bank(b), AF.Identity, [], ["ps%d" % b, "hb%d" % b], scale=0.5)
+    def times(out, a, c, rd, wr):
+        op("s", lambda: S.activation(out, a, AF.Identity, scale=c), rd, wr, cost=PLAIN, other=("v", lambda: V.tensor_scalar(out, a, c, None, O.mult)))
+
+    def halves():
+        for b in range(4): times(T.hb[:, C * b:C * b + C], bank(b), 0.5, [], ["ps%d" % b, "hb%d" % b])
 
     def aside():
         for b in range(4):
-            act(T.ga[:, C * b:C * b + C], T.hb[:, C * b:C * b + C].indirect(T.xw0[:]), AF.Copy, ["hb%d" % b, "xw0"], ["ga%d" % b])
+            either(T.ga[:, C * b:C * b + C], T.hb[:, C * b:C * b + C].indirect(T.xw0[:]), ["hb%d" % b, "xw0"], ["ga%d" % b])
 
     def prepare():
         ts(T.ka[:], T.dif[:], 0.0, None, O.not_equal, None, ["dif"], ["ka"])
         ts(T.kb[:], T.dif[:], 1.0, GAIN - 1.0, O.is_equal, O.mult, ["dif"], ["kb"])
         tt(T.hm[:, 0:C], T.ka[:], T.kb[:], O.add, ["ka", "kb"], ["hm"])
         cp(T.hm[:, C:2 * C], T.hm[:, 0:C], ["hm"], ["hm"])
-        cp(T.hh[:, C:2 * C], T.hh[:, 0:C], ["hh"], ["hh"])
-        cp(T.cc[:, C:2 * C], T.cc[:, 0:C], ["cc"], ["cc"])
         ts(T.com[:], T.pf[:], 15.0, 1.0 / GAIN, O.is_ge, O.max, ["pf"], ["com"])
-        op("v", lambda: V.memset(T.ones[:], 1.0), [], ["ones"])
-        op("v", lambda: V.memset(T.onf[:], 1.0), [], ["onf"])
-        op("v", lambda: V.memset(T.buf[:], 0.0), [], ["buf"])
 
     def prepare2():
         ts(T.cw[:], T.cw0[:], T.pf[:, 0:1], None, O.add, None, ["cw0", "pf"], ["cw"])
-        cp(T.muw[:], T.mi[:], ["mi"], ["muw"])
-        cp(T.muf[:], T.mi[:], ["mi"], ["muf"])
-        tt(T.dmw[:], T.muf[:], T.cw[:], O.subtract, ["muf", "cw"], ["dmw"])
+        tt(T.dmw[:], T.mi[:], T.cw[:], O.subtract, ["mi", "cw"], ["dmw"])
+        for w, o in (("low", O.min), ("hiw", O.max)):
+            tt(T.muf[:], T.mi[:], T.cw[:], o, ["mi", "cw"], ["muf"])
+            cp(T[w][:], T.muf[:], ["muf"], [w])
 
     def first():
-        cp(T.ou[:], T.ou0[:], ["ou0"], ["ou"])
         quant("uq", "up", "ut", 128)
         cp(T.ur[:].bitcast(dt.uint32), T.uq[:].bitcast(dt.uint32).indirect(T.ou[:]), ["uq", "ou"], ["ur"])
         cp(T.urp[:], T.up[:].indirect(T.ou[:]), ["up", "ou"], ["urp"])
@@ -248,15 +300,15 @@ def rank_program(g, core, T, topo):
 
     def constants():
         for b in range(4):
-            op("v", lambda: V.quantize_mx(T.eq[:, 128 * b:128 * b + 128], T.ep[:, 128 * b:128 * b + 128], T.et[:, 512 * b:512 * b + 512]), ["et%d" % b], ["eq", "ep"])
+            op("v", lambda b=b: V.quantize_mx(T.eq[:, 128 * b:128 * b + 128], T.ep[:, 128 * b:128 * b + 128], T.et[:, 512 * b:512 * b + 512]), ["et%d" % b], ["eq%d" % b], cost=0.15)
         products()
 
-    def lastly():
-        quant("vq", "vp", "vt", 128)
-        halves()
-        aside()
-
-    jump({0: prepare, 1: prepare2, 2: first, 3: constants, 8: lastly})
+    first()
+    constants()
+    jump()
+    prepare()
+    prepare2()
+    quant("vq", "vp", "vt", 128)
 
     qcur = ["qa", "qb"]
     for k, step in enumerate(STEPS):
@@ -265,17 +317,16 @@ def rank_program(g, core, T, topo):
         rid, pid = topo.addr(peer, core)
         mask = topo.mask(core, peer)
         width = len(topo.engines(core, peer))
-        ts(T.nf[:], bank(4), 0.0, None, O.is_ge, None, [], ["ps4", "nf"])
-        cp(T.g2[:, 0:C], T.nf[:].indirect(T.linw[:, 0:K]), ["nf", "linw"], ["g2a"])
-        act(T.g2[:, C:2 * C], T.nf[:].indirect(T.linw[:, K:2 * K]), AF.Copy, ["nf", "linw"], ["g2b"])
-        act(T.ss[:], bank(4), AF.Copy, [], ["ps4", "ss"])
+        ts(T.nf[:], bank(4), 0.0, None, O.is_ge, None, [], ["ps4", "nf"], PLAIN)
+        cp(T.g2[:, 0:16 * CUT], T.nf[:].indirect(T.linw[:, 0:CUT]), ["nf", "linw"], ["g2a"], GATHER * CUT / K)
+        act(T.g2[:, 16 * CUT:2 * C], T.nf[:].indirect(T.linw[:, CUT:2 * K]), AF.Copy, ["nf", "linw"], ["g2b"], cost=GATHER * (2 * K - CUT) / K)
+        act(T.ss[:], bank(4), AF.Copy, [], ["ps4", "ss"], cost=PLAIN)
         scan(T.fs[:], T.g2[:], T.ones[:], 1.0, O.mult, O.add, ["g2a", "g2b", "ones"], ["fs"])
         act(T.ij[:, 0:C], T.fs[:].indirect(T.pos[:, K:2 * K]), AF.Copy, ["fs", "pos"], ["ija"])
         scan(T.rs[:], T.g2[:, ::-1], T.ones[:], 1.0, O.mult, O.add, ["g2a", "g2b", "ones"], ["rs"])
-        cp(T.ij[:, C:2 * C], T.rs[:].indirect(T.posr[:]), ["rs", "posr"], ["ijb"])
-        if k:
-            halves()
-            aside()
+        cp(T.ij[:, C:2 * C], T.rs[:].indirect(T.posr[:]), ["rs", "posr"], ["ijb"], GATHER)
+        halves()
+        aside()
         scan(T.eij[:], T.hm[:], T.ij[:], 1.0, O.mult, O.max, ["hm", "ija", "ijb"], ["eij"])
         ts(T.k2[:], T.eij[:, 15:2 * C:16], T.com[:, 0:1], None, O.mult, None, ["eij", "com"], ["k2"])
         tt(T.k3[:], T.k2[:], T.ll[:], O.min, ["k2", "ll", "lm"], ["k3"])
@@ -285,78 +336,81 @@ def rank_program(g, core, T, topo):
         tt(T.zm[:], T.zl[:], T.ll[:, 0:K], O.mult, ["zl", "ll"], ["zm"])
         tt(T.of[:], T.zm[:], T.dp[:], O.add, ["zm", "dp"], ["of"])
         cp(T.ow[:], T.of[:], ["of"], ["ow"])
-        cp(T.mf[:], T.lin[:].indirect(T.ow[:]), ["lin", "ow"], ["mf"])
+        either(T.mf[:], T.lin[:].indirect(T.ow[:]), ["lin", "ow"], ["mf"])
         unwrap("mf", C, "mw")
         for b in range(4):
-            tt(T.zt[:, b:4 * C:4], T.hb[:, C * b:C * b + C].indirect(T.mw[:]), T.ga[:, C * b:C * b + C], O.add, ["hb%d" % b, "mw", "ga%d" % b], ["zt"])
+            tt(T.zt[:, b:4 * C:4], T.hb[:, C * b:C * b + C].indirect(T.mw[:]), T.ga[:, C * b:C * b + C], O.add, ["hb%d" % b, "mw", "ga%d" % b], ["zt%d" % b], GATHER)
             if b == 0:
                 act(T.st[:], T.ss[:].indirect(T.mw[:]), AF.Copy, ["ss", "mw"], ["st"])
-                act(T.su[:], T.st[:], AF.Copy, ["st"], ["su"])
-        quant("zq", "zp", "zt", C)
-        settle("g", {last["zq"], last["zp"]})
-        land, sent = T.sem["arr%d" % k], T.sem["snt%d" % k]
-        g.remote_dma(T["rq%d" % k][:].bitcast(dt.uint8), T.zq[:].bitcast(dt.uint8), land, sent, pid, rid, mask)
-        g.remote_dma(T["rp%d" % k][:], T.zp[:], land, sent, pid, rid, mask)
-        for a in ("zq", "zp"): readers.setdefault(a, set()).add(("snt%d" % k, 2 * width))
-        for a in ("rq%d" % k, "rp%d" % k): last[a] = ("arr%d" % k, 2 * width)
-        count["arr%d" % k] = count["snt%d" % k] = 2 * width
-        tt(T.sd[:], T.st[:].indirect(T.muw[:]), T.su[:], O.subtract, ["st", "muw", "su"], ["sd"])
-        act(T.sg[:], T.sd[:], AF.Sign, ["sd"], ["sg"])
-        scan(T.eh[:, 0:C], T.hh[:, 0:C], T.sg[:], 0.0, O.add, O.max, ["hh", "sg"], ["eh"])
+                act(T.su[:], T.st[:].indirect(T.low[:]), AF.Copy, ["st", "low"], ["su"])
+        quant("zq", "zp", "zt", C, ["zt0", "zt1", "zt2", "zt3"])
+
+        def send(k=k, pid=pid, rid=rid, mask=mask, n=2 * width):
+            settle("g", {last["zq"], last["zp"]})
+            land, sent = T.sem["arr%d" % k], T.sem["snt%d" % k]
+            g.remote_dma(T["rq%d" % k][:].bitcast(dt.uint8), T.zq[:].bitcast(dt.uint8), land, sent, pid, rid, mask)
+            g.remote_dma(T["rp%d" % k][:], T.zp[:], land, sent, pid, rid, mask)
+            for a in ("zq", "zp"): readers.setdefault(a, set()).add(("snt%d" % k, n))
+            for a in ("rq%d" % k, "rp%d" % k): last[a] = ("arr%d" % k, n)
+            count["arr%d" % k] = count["snt%d" % k] = n
+
+        op("g", None, ["zq", "zp"], ["rq%d" % k, "rp%d" % k], cost=0.6, lat=FLIGHT, send=send)
+        tt(T.sg[:], T.st[:].indirect(T.hiw[:]), T.su[:], O.is_lt, ["st", "hiw", "su"], ["sg"], GATHER)
+        scan(T.eh[:, 0:C], T.hh[:, 0:C], T.sg[:], 0.0, O.add, O.max, ["hh", "sg"], ["eh"], HALF)
         ts(T.de[:], T.eh[:, 15:C:16], T.coh[:, 0:1], float(MID), O.subtract, O.subtract, ["eh", "coh"], ["de"])
-        tt(T.dp[:], T.de[:], T.dmw[:], O.mult, ["de", "dmw"], ["dp"])
-        ts(T.zl[:], T.dp[:], 0.0, None, O.is_lt, None, ["dp"], ["zl"])
-        tt(T.zm[:], T.zl[:], T.dmw[:], O.mult, ["zl", "dmw"], ["zm"])
+        tt(T.zm[:], T.de[:], T.dmw[:], O.mult, ["de", "dmw"], ["zm"])
         tt(T.of[:], T.zm[:], T.cw[:], O.add, ["zm", "cw"], ["of"])
         cp(T.sw[:], T.of[:], ["of"], ["sw"])
         qo, qn = qcur[k % 2], qcur[1 - k % 2]
-        cp(T.yf[:], T[qo][:].indirect(T.sw[:]), [qo, "sw"], ["yf"])
-        act(T.sf[:], T.cc[:, 0:C].indirect(T.sw[:]), AF.Copy, ["cc", "sw"], ["sf"])
+        either(T.yf[:], T[qo][:].indirect(T.sw[:]), [qo, "sw"], ["yf"])
+        either(T.sf[:], T.cc[:, 0:C].indirect(T.sw[:]), ["cc", "sw"], ["sf"])
         unwrap("yf", C, "yw")
-        cp(T[qn][:], T.sf[:].indirect(T.yw[:]), ["sf", "yw"], [qn])
+        either(T[qn][:], T.sf[:].indirect(T.yw[:]), ["sf", "yw"], [qn])
         if not final:
-            cp(T.xf0[:], T[qn][:].indirect(T.pw[:]), [qn, "pw"], ["xf0"])
+            either(T.xf0[:], T[qn][:].indirect(T.pw[:]), [qn, "pw"], ["xf0"])
         else:
-            ts(T.dd[:], T[qn][:], float(MID), None, O.add, None, [qn], ["dd"])
-            op("y", lambda: g.sync.dma_start(T.qo[:], T.dd[0:128:16, :]), ["dd"], [], "st_oq", 16)
+            ts(T.dd[:], T[qn][:], float(MID), None, O.add, None, [qn], ["dd"], PLAIN)
+            op("y", lambda: g.sync.dma_start(T.qo[:], T.dd[0:128:16, :]), ["dd"], [], "st_oq", 16, lat=2.5)
 
         def layer():
             for b in range(4): mm((5, 6, 7, 4)[b], "wq", "wp", 128 * b, "rq%d" % k, "rp%d" % k)
 
         def scaled(bs):
             for b in bs:
-                act(T.rb[:, C * b:C * b + C], bank((5, 6, 7, 4)[b]), AF.Identity, [], ["ps%d" % (5, 6, 7, 4)[b], "rb%d" % b], scale=0.03125)
+                times(T.rb[:, C * b:C * b + C], bank((5, 6, 7, 4)[b]), 0.03125, [], ["ps%d" % (5, 6, 7, 4)[b], "rb%d" % b])
 
         def picked(bs):
             for b in bs:
-                act(T.mb[:, C * b:C * b + C], T.rb[:, C * b:C * b + C].indirect(T.mw[:]), AF.Copy, ["rb%d" % b, "mw"], ["mb%d" % b])
+                either(T.mb[:, C * b:C * b + C], T.rb[:, C * b:C * b + C].indirect(T.mw[:]), ["rb%d" % b, "mw"], ["mb%d" % b])
 
         def added(bs=range(4)):
             for b in bs:
-                tt(T.xt[:, b:4 * C:4], T.mb[:, C * b:C * b + C], bank(b), O.add, ["mb%d" % b], ["ps%d" % b, "xt"])
-            quant("tq", "tp", "xt", C)
+                tt(T.xt[:, b:4 * C:4], T.mb[:, C * b:C * b + C], bank(b), O.add, ["mb%d" % b], ["ps%d" % b, "xt%d" % b], PLAIN)
+            quant("tq", "tp", "xt", C, ["xt", "xt0", "xt1", "xt2", "xt3"])
 
         if not final:
-            def after_scatter():
-                added()
-                products()
-            jump({0: layer, 5: lambda: scaled([0]), 6: lambda: scaled([1]), 7: lambda: scaled([2]),
-                  8: lambda: (scaled([3]), picked(range(4))), 9: after_scatter})
+            layer()
+            scaled(range(4))
+            picked(range(4))
+            added()
+            products()
+            jump()
         else:
             layer()
             for b in (0, 1):
-                cp(T.ga[:, C * b:C * b + C], bank(b), [], ["ps%d" % b, "ga%d" % b])
-            for b, n in ((0, 5), (1, 6)):
-                ts(T.rb[:, C * b:C * b + C], bank(n), 0.03125, None, O.mult, None, [], ["ps%d" % n, "rb%d" % b])
-            scaled([2, 3])
+                cp(T.ga[:, C * b:C * b + C], bank(b), [], ["ps%d" % b, "ga%d" % b], PLAIN)
+            scaled(range(4))
             picked([2, 3])
             for b in (0, 1):
-                tt(T.xt[:, b:4 * C:4], T.rb[:, C * b:C * b + C].indirect(T.mw[:]), T.ga[:, C * b:C * b + C], O.add, ["rb%d" % b, "mw", "ga%d" % b], ["xt"])
+                tt(T.xt[:, b:4 * C:4], T.rb[:, C * b:C * b + C].indirect(T.mw[:]), T.ga[:, C * b:C * b + C], O.add, ["rb%d" % b, "mw", "ga%d" % b], ["xt%d" % b], GATHER)
             added([2, 3])
-            op("y", lambda: g.sync.dma_start(T.oc[:], T.tq[:].bitcast(dt.uint8)), ["tq"], [], "st_occ", 16)
+            op("y", lambda: g.sync.dma_start(T.oc[:], T.tq[:].bitcast(dt.uint8)), ["tq"], [], "st_occ", 16, lat=2.5)
             for a in range(4):
-                op("y", lambda: g.sync.dma_start(T.osc[4 * a:4 * a + 4, :], T.tp[32 * a:32 * a + 4, :]), ["tp"], [], "st_oss", 16)
+                op("y", lambda a=a: g.sync.dma_start(T.osc[4 * a:4 * a + 4, :], T.tp[32 * a:32 * a + 4, :]), ["tp"], [], "st_oss", 16, lat=2.5)
             mm(4, "vq", "vp", 0, "tq", "tp")
-            act(T.yo[:], bank(4), AF.Copy, [], ["ps4", "yo"])
-            op("y", lambda: g.sync.dma_start(T.y[:], T.yo[:]), ["yo"], [], "st_oy", 16)
+            act(T.yo[:], bank(4), AF.Copy, [], ["ps4", "yo"], cost=PLAIN)
+            op("y", lambda: g.sync.dma_start(T.y[:], T.yo[:]), ["yo"], [], "st_oy", 16, lat=2.5)
+    for n, e in ordered():
+        if n["send"]: n["send"]()
+        else: issue(n, e)
     settle("g", set(count.items()))

@@ -6,8 +6,8 @@ K = C // 16
 STEPS = [1, 2, 4]
 JUMPS = [(0, 1), (1, 2), (2, 4), (3, 8), (4, 16), (4, 16), (5, 32), (6, 64)]
 SEEN = 143
-CUT = 20
-TINY, PLAIN, HALF, GATHER, SCATTER, NEAR, WAKE, BIAS, LOOK, SLACK, FLIGHT = 0.09, 0.31, 0.17, 0.52, 2.2, 0.08, 0.16, 0.5, 0.5, 0.1, 6.0
+CUT = 18
+TINY, PLAIN, HALF, GATHER, SCATTER, NEAR, WAKE, BIAS, LOOK, SLACK, FLIGHT = 0.082, 0.31, 0.232, 0.488, 2.082, 0.064, 0.191, 0.555, 0.402, 0.094, 5.5
 MID = 144
 UNIT, LIFT = 512, 8
 HOLD, DROP = float(2 ** 19), float(-2 ** 21)
@@ -28,19 +28,18 @@ SCRATCH = {
     "tq": sb(C, MX), "tp": sb(C, U8), "zq": sb(C, MX), "zp": sb(C, U8),
     "et": sb(2048, BF), "one": sb(512, BF), "zt": sb(4 * C, BF),
     "cc": sb(2 * C, BF), "tm": sb(C, F32), "dif": sb(C, F32), "ka": sb(C, F32), "kb": sb(C, F32),
-    "hc": sb(C, F32), "hh": sb(2 * C, F16), "hm": sb(2 * C, BF), "ones": sb(2 * C, BF),
-    "onf": sb(C, F32),
-    "pp": sb(1, I32), "pm": sb(1, I32), "pf": sb(1, F32), "cor": sb(1, F32), "com": sb(1, F32), "coh": sb(1, F32),
+    "hc": sb(C, F32), "hh": sb(2 * C, F16), "hm": sb(2 * C, F16), "ones": sb(2 * C, BF),
+    "pp": sb(1, I32), "pm": sb(1, I32), "pf": sb(1, F32), "cor": sb(1, F32), "coj": sb(1, F32), "coh": sb(1, F32),
     "cw0": sb(K, F32), "cw": sb(K, F32), "ou0": sb(8, I32), "ou": sb(8, U16),
     "w0": sb(C, F32), "wm0": sb(C, F32), "cd": sb(C, F32),
     "pw": sb(K, U16), "qw": sb(K, U16), "low": sb(K, U16), "hiw": sb(K, U16), "dmw": sb(K, F32), "muf": sb(K, F32),
     "qa": sb(C, BF), "qb": sb(C, BF), "ex": sb(C, F32), "eh": sb(2 * C, F16),
     "wa": sb(C, F32), "wb": sb(C, F32), "wm": sb(C, F32),
-    "dd": sb(C, F32), "ctr": sb(C, F32), "c5": sb(C, F32), "buf": sb(C + 8, F32), "bg": sb(C, F32), "comb": sb(C, F32),
-    "vi": sb(K, I32), "li": sb(K, I32), "lw": sb(K, U16), "tw": sb(K, I32), "ci": sb(K, I32), "t2": sb(K, F32), "ll": sb(2 * K, I32),
-    "ps2": sb(2 * K, I32), "pos": sb(2 * K, U16), "posr": sb(K, U16), "lin": sb(2 * C, BF), "linw": sb(2 * K, U16),
-    "nf": sb(C, BF), "ss": sb(C, F32), "g2": sb(2 * C, BF), "fs": sb(2 * C, BF), "rs": sb(2 * C, BF), "ij": sb(2 * C, BF), "eij": sb(2 * C, BF),
-    "k2": sb(2 * K, F32), "k3": sb(2 * K, F32), "de": sb(K, F32), "zl": sb(K, F32), "zm": sb(K, F32), "dp": sb(K, F32), "of": sb(K, F32), "ow": sb(K, U16),
+    "dd": sb(C, F32), "ctr": sb(C, F32), "c5": sb(C, F32), "buf": sb(C + 8, F32), "bg": sb(C, F32), "lg": sb(C, BF),
+    "vi": sb(K, I32), "lw": sb(K, U16), "tw": sb(K, I32), "t2": sb(K, F32), "ll": sb(K, F32),
+    "ps2": sb(2 * K, F32), "pos": sb(2 * K, U16), "posr": sb(K, U16), "lin": sb(2 * C, BF), "linw": sb(2 * K, U16),
+    "nf": sb(C, BF), "ss": sb(C, F32), "g2": sb(2 * C, BF), "fs": sb(2 * C, BF), "rs": sb(2 * C, BF), "ij": sb(2 * C, BF), "eij": sb(2 * C, F16),
+    "cq": sb(K, F32), "lc": sb(2 * K, F32), "k3": sb(2 * K, F32), "de": sb(K, F32), "zl": sb(K, F32), "zm": sb(K, F32), "dp": sb(K, F32), "of": sb(K, F32), "ow": sb(K, U16),
     "mf": sb(C, BF), "mw": sb(K, U16),
     "st": sb(C, F32), "su": sb(C, F32), "sg": sb(C, BF),
     "sw": sb(K, U16), "sf": sb(C, BF), "yf": sb(C, BF), "yw": sb(K, U16),
@@ -222,8 +221,7 @@ def rank_program(g, core, T, topo):
     act(T.qa[:], T.cc[:, 0:C].indirect(T.qw[:]), AF.Copy, ["cc", "qw"], ["qa"])
     act(T.xf0[:], T.qa[:].indirect(T.pw[:]), AF.Copy, ["qa", "pw"], ["xf0"])
     op("v", lambda: V.memset(T.ones[:], 1.0), [], ["ones"], cost=PLAIN)
-    op("v", lambda: V.memset(T.onf[:], 1.0), [], ["onf"], cost=PLAIN)
-    op("v", lambda: V.memset(T.buf[:], 0.0), [], ["buf"], cost=PLAIN)
+    op("v", lambda: V.memset(T.buf[:, 0:8], 0.0), [], ["buf"])
     cp(T.cc[:, C:2 * C], T.cc[:, 0:C], ["cc"], ["cd2"], HALF)
     cp(T.hh[:, C:2 * C], T.hh[:, 0:C], ["hh"], ["hh2"], HALF)
     cp(T.ou[:], T.ou0[:], ["ou0"], ["ou"])
@@ -243,24 +241,25 @@ def rank_program(g, core, T, topo):
                 unwrap("xf%d" % (k + 1), C, "xw%d" % (k + 1))
                 made = k + 1
         tt(T.dd[:], T[w][:].indirect(T.xw0[:]), T.cd[:], O.subtract, [w, "xw0", "cd"], ["dd"], GATHER)
-        act(T.c5[:], T.dd[:], AF.Relu, ["dd"], ["c5"], scale=512.0)
-        act(T.ctr[:], T.dd[:], AF.Relu, ["dd"], ["ctr"], cost=PLAIN)
+        for a, c in (("c5", 2.0), ("ctr", 1.0)):
+            op("s", lambda a=a, c=c: S.activation(T[a][:], T.dd[:], AF.Relu, scale=c), ["dd"], [a], cost=PLAIN,
+               other=("v", lambda a=a, c=c: V.tensor_scalar(T[a][:], T.dd[:], 0.0, c, O.max, O.mult)))
         a = held(w)
         ts(T.lw[:], a, T.cor[:, 0:1], 1.0 / UNIT, O.subtract, O.mult, ["ex", "cor"], ["lw"])
         ts(T.vi[:], a, T.cor[:, 0:1], float(LIFT), O.subtract, O.subtract, ["ex", "cor"], ["vi"])
-        scan(T.buf[:, 1:C + 1], T.onf[:], T.c5[:], 0.0, O.mult, O.add, ["onf", "c5"], ["buf"])
+        scan(T.buf[:, 1:C + 1], T.ones[:, 0:C], T.c5[:], 0.0, O.mult, O.add, ["ones", "c5"], ["buf"])
         either(T.bg[:], T.buf[:, 0:C].indirect(T.lw[:]), ["buf", "lw"], ["bg"])
         ts(T.tw[:], T.vi[:], UNIT - 1, None, O.bitwise_and, None, ["vi"], ["tw"])
-        ts(T.t2[:], T.tw[:], 256.0, T.cor[:, 0:1], O.mult, O.subtract, ["tw", "cor"], ["t2"])
-        tt(T.comb[:], T.ctr[:].indirect(T.lw[:]), T.bg[:], O.add, ["ctr", "lw", "bg"], ["comb"], GATHER)
-        a = held("comb")
-        tt(T.ci[:], a, T.t2[:], O.add, ["ex", "t2"], ["ci"])
-        ts(T.ps2[:, 0:K], T.ci[:], 8, None, O.arith_shift_right, None, ["ci"], ["psa"])
-        ts(T.ll[:, 0:K], T.ci[:], 255, None, O.bitwise_and, None, ["ci"], ["ll"])
+        ts(T.t2[:], T.tw[:], T.cor[:, 0:1], None, O.subtract, None, ["tw", "cor"], ["t2"])
+        either(T.lg[:], T.ctr[:].indirect(T.lw[:]), ["ctr", "lw"], ["lg"])
+        scan(T.eh[:, 0:C], T.hh[:, 0:C], T.lg[:], 0.0, O.add, O.max, ["hh", "lg"], ["eh"], HALF)
+        ts(T.ll[:], T.eh[:, 15:C:16], T.coh[:, 0:1], float(MID), O.subtract, O.subtract, ["eh", "coh"], ["ll"])
+        a = held("bg")
+        tt(T.ps2[:, 0:K], a, T.t2[:], O.add, ["ex", "t2"], ["psa"])
         tt(T.ps2[:, K:2 * K], T.ps2[:, 0:K], T.ll[:, 0:K], O.add, ["psa", "ll"], ["psb"])
         cp(T.pos[:], T.ps2[:], ["psa", "psb"], ["pos"])
         cp(T.lin[:].indirect(T.pos[:]), T.cc[:], ["pos", "cc", "cd2"], ["lin"], SCATTER)
-        ts(T.ll[:, K:2 * K], T.ci[:], 255, None, O.bitwise_and, None, ["ci"], ["lm"])
+        for a, w in ((0, "lca"), (K, "lcb")): ts(T.lc[:, a:a + K], T.ll[:], T.coj[:, 0:1], None, O.add, None, ["ll", "coj"], [w])
         ts(T.posr[:], T.ps2[:, 0:K], -1.0, float(2 * C - 1), O.mult, O.add, ["psa"], ["posr"])
         unwrap("lin", 2 * C, "linw", ["hh2"])
 
@@ -276,18 +275,17 @@ def rank_program(g, core, T, topo):
 
     def aside():
         for b in range(4):
-            either(T.ga[:, C * b:C * b + C], T.hb[:, C * b:C * b + C].indirect(T.xw0[:]), ["hb%d" % b, "xw0"], ["ga%d" % b])
+            either(T.ga[:, b:4 * C:4], T.hb[:, C * b:C * b + C].indirect(T.xw0[:]), ["hb%d" % b, "xw0"], ["ga%d" % b])
 
     def prepare():
-        ts(T.ka[:], T.dif[:], 0.0, None, O.not_equal, None, ["dif"], ["ka"])
-        ts(T.kb[:], T.dif[:], 1.0, GAIN - 1.0, O.is_equal, O.mult, ["dif"], ["kb"])
-        tt(T.hm[:, 0:C], T.ka[:], T.kb[:], O.add, ["ka", "kb"], ["hm"])
-        cp(T.hm[:, C:2 * C], T.hm[:, 0:C], ["hm"], ["hm"])
-        ts(T.com[:], T.pf[:], 15.0, 1.0 / GAIN, O.is_ge, O.max, ["pf"], ["com"])
+        ts(T.hm[:], T.hh[:], 2.0, None, O.mult, None, ["hh", "hh2"], ["hm"], PLAIN)
+        ts(T.coj[:], T.cor[:], 2.0 ** -9, None, O.mult, None, ["cor"], ["coj"])
 
     def prepare2():
         ts(T.cw[:], T.cw0[:], T.pf[:, 0:1], None, O.add, None, ["cw0", "pf"], ["cw"])
         tt(T.dmw[:], T.mi[:], T.cw[:], O.subtract, ["mi", "cw"], ["dmw"])
+        ts(T.muf[:], T.dmw[:], T.cor[:, 0:1], 2.0 ** -10, O.mult, O.mult, ["dmw", "cor"], ["muf"])
+        tt(T.cq[:], T.cw[:], T.muf[:], O.subtract, ["cw", "muf"], ["cq"])
         for w, o in (("low", O.min), ("hiw", O.max)):
             tt(T.muf[:], T.mi[:], T.cw[:], o, ["mi", "cw"], ["muf"])
             cp(T[w][:], T.muf[:], ["muf"], [w])
@@ -305,9 +303,9 @@ def rank_program(g, core, T, topo):
 
     first()
     constants()
-    jump()
     prepare()
     prepare2()
+    jump()
     quant("vq", "vp", "vt", 128)
 
     qcur = ["qa", "qb"]
@@ -327,9 +325,8 @@ def rank_program(g, core, T, topo):
         cp(T.ij[:, C:2 * C], T.rs[:].indirect(T.posr[:]), ["rs", "posr"], ["ijb"], GATHER)
         halves()
         aside()
-        scan(T.eij[:], T.hm[:], T.ij[:], 1.0, O.mult, O.max, ["hm", "ija", "ijb"], ["eij"])
-        ts(T.k2[:], T.eij[:, 15:2 * C:16], T.com[:, 0:1], None, O.mult, None, ["eij", "com"], ["k2"])
-        tt(T.k3[:], T.k2[:], T.ll[:], O.min, ["k2", "ll", "lm"], ["k3"])
+        scan(T.eij[:], T.hm[:], T.ij[:], 0.0, O.add, O.max, ["hm", "ija", "ijb"], ["eij"])
+        tt(T.k3[:], T.eij[:, 15:2 * C:16], T.lc[:], O.min, ["eij", "lca", "lcb"], ["k3"])
         tt(T.de[:], T.k3[:, K:2 * K], T.k3[:, 0:K], O.subtract, ["k3"], ["de"])
         ts(T.zl[:], T.de[:], 0.0, None, O.is_lt, None, ["de"], ["zl"])
         tt(T.dp[:], T.de[:], T.ps2[:, 0:K], O.add, ["de", "psa"], ["dp"])
@@ -338,28 +335,30 @@ def rank_program(g, core, T, topo):
         cp(T.ow[:], T.of[:], ["of"], ["ow"])
         either(T.mf[:], T.lin[:].indirect(T.ow[:]), ["lin", "ow"], ["mf"])
         unwrap("mf", C, "mw")
-        for b in range(4):
-            tt(T.zt[:, b:4 * C:4], T.hb[:, C * b:C * b + C].indirect(T.mw[:]), T.ga[:, C * b:C * b + C], O.add, ["hb%d" % b, "mw", "ga%d" % b], ["zt%d" % b], GATHER)
-            if b == 0:
-                act(T.st[:], T.ss[:].indirect(T.mw[:]), AF.Copy, ["ss", "mw"], ["st"])
-                act(T.su[:], T.st[:].indirect(T.low[:]), AF.Copy, ["st", "low"], ["su"])
-        quant("zq", "zp", "zt", C, ["zt0", "zt1", "zt2", "zt3"])
+        act(T.st[:], T.ss[:].indirect(T.mw[:]), AF.Copy, ["ss", "mw"], ["st"])
+        act(T.su[:], T.st[:].indirect(T.low[:]), AF.Copy, ["st", "low"], ["su"])
+        parts = [(0, 8), (8, K)] if final else [(0, K)]
+        for h, (a, z) in enumerate(parts):
+            own = [h] if final else [0, 1]
+            zs = ["zt%d%d" % (j, b) for b in range(4) for j in own]
+            for b in range(4):
+                tt(T.zt[:, 64 * a + b:64 * z:4], T.hb[:, C * b:C * b + C].indirect(T.mw[:, a:z]), T.ga[:, 64 * a + b:64 * z:4], O.add, ["hb%d" % b, "mw", "ga%d" % b], ["zt%d%d" % (j, b) for j in own], GATHER * (z - a) / K)
+            op("v", lambda a=a, z=z: V.quantize_mx(T.zq[:, 16 * a:16 * z], T.zp[:, 16 * a:16 * z], T.zt[:, 64 * a:64 * z]), zs, ["zq0", "zq1"][h:], cost=0.32 * (z - a) / K)
 
-        def send(k=k, pid=pid, rid=rid, mask=mask, n=2 * width):
-            settle("g", {last["zq"], last["zp"]})
-            land, sent = T.sem["arr%d" % k], T.sem["snt%d" % k]
-            g.remote_dma(T["rq%d" % k][:].bitcast(dt.uint8), T.zq[:].bitcast(dt.uint8), land, sent, pid, rid, mask)
-            g.remote_dma(T["rp%d" % k][:], T.zp[:], land, sent, pid, rid, mask)
-            for a in ("zq", "zp"): readers.setdefault(a, set()).add(("snt%d" % k, n))
-            for a in ("rq%d" % k, "rp%d" % k): last[a] = ("arr%d" % k, n)
-            count["arr%d" % k] = count["snt%d" % k] = n
+            def send(k=k, pid=pid, rid=rid, mask=mask, a=16 * a, z=16 * z, h=h, n=2 * width * len(parts)):
+                settle("g", {last["zq%d" % h]})
+                land, sent = T.sem["arr%d" % k], T.sem["snt%d" % k]
+                g.remote_dma(T["rq%d" % k][:, a:z].bitcast(dt.uint8), T.zq[:, a:z].bitcast(dt.uint8), land, sent, pid, rid, mask)
+                g.remote_dma(T["rp%d" % k][:, a:z], T.zp[:, a:z], land, sent, pid, rid, mask)
+                readers.setdefault("zq%d" % h, set()).add(("snt%d" % k, n))
+                for r in ("rq%d" % k, "rp%d" % k): last[r] = ("arr%d" % k, n)
+                count["arr%d" % k] = count["snt%d" % k] = n
 
-        op("g", None, ["zq", "zp"], ["rq%d" % k, "rp%d" % k], cost=0.6, lat=FLIGHT, send=send)
+            op("g", None, ["zq%d" % h], ["rq%d" % k, "rp%d" % k], cost=0.6, lat=FLIGHT, send=send)
         tt(T.sg[:], T.st[:].indirect(T.hiw[:]), T.su[:], O.is_lt, ["st", "hiw", "su"], ["sg"], GATHER)
         scan(T.eh[:, 0:C], T.hh[:, 0:C], T.sg[:], 0.0, O.add, O.max, ["hh", "sg"], ["eh"], HALF)
-        ts(T.de[:], T.eh[:, 15:C:16], T.coh[:, 0:1], float(MID), O.subtract, O.subtract, ["eh", "coh"], ["de"])
-        tt(T.zm[:], T.de[:], T.dmw[:], O.mult, ["de", "dmw"], ["zm"])
-        tt(T.of[:], T.zm[:], T.cw[:], O.add, ["zm", "cw"], ["of"])
+        tt(T.zm[:], T.eh[:, 15:C:16], T.dmw[:], O.mult, ["eh", "dmw"], ["zm"])
+        tt(T.of[:], T.zm[:], T.cq[:], O.add, ["zm", "cq"], ["of"])
         cp(T.sw[:], T.of[:], ["of"], ["sw"])
         qo, qn = qcur[k % 2], qcur[1 - k % 2]
         either(T.yf[:], T[qo][:].indirect(T.sw[:]), [qo, "sw"], ["yf"])
@@ -398,11 +397,11 @@ def rank_program(g, core, T, topo):
         else:
             layer()
             for b in (0, 1):
-                cp(T.ga[:, C * b:C * b + C], bank(b), [], ["ps%d" % b, "ga%d" % b], PLAIN)
+                cp(T.mb[:, C * b:C * b + C], bank(b), [], ["ps%d" % b, "mb%d" % b], PLAIN)
             scaled(range(4))
             picked([2, 3])
             for b in (0, 1):
-                tt(T.xt[:, b:4 * C:4], T.rb[:, C * b:C * b + C].indirect(T.mw[:]), T.ga[:, C * b:C * b + C], O.add, ["rb%d" % b, "mw", "ga%d" % b], ["xt%d" % b], GATHER)
+                tt(T.xt[:, b:4 * C:4], T.rb[:, C * b:C * b + C].indirect(T.mw[:]), T.mb[:, C * b:C * b + C], O.add, ["rb%d" % b, "mw", "mb%d" % b], ["xt%d" % b], GATHER)
             added([2, 3])
             op("y", lambda: g.sync.dma_start(T.oc[:], T.tq[:].bitcast(dt.uint8)), ["tq"], [], "st_occ", 16, lat=2.5)
             for a in range(4):

from concourse.bass import DstId, RemoteDMATransfer
from concourse.mybir import dt, AluOpType as O, ActivationFunctionType as AF

C = 288
K = C // 16
STEPS = [1, 2, 4]
JUMPS = [(0, 1), (1, 2), (2, 4), (3, 8), (4, 16), (4, 16), (5, 32), (6, 64)]
SEEN = 143
CUT = 18
TINY, PLAIN, HALF, GATHER, SCATTER, NEAR, WAKE, BIAS, LOOK, SLACK, FLIGHT = 0.082, 0.31, 0.232, 0.488, 2.082, 0.064, 0.191, 0.555, 0.402, 0.094, 5.5
MID = 144
UNIT, LIFT = 512, 8
HOLD, DROP = float(2 ** 19), float(-2 ** 21)
GAIN = float(2 ** 20)

F32, BF, F16, I32, U16, U8, MX = "float32", "bfloat16", "float16", "int32", "uint16", "uint8", "float8_e4m3fn_x4"


def sb(n, d):
    return ("sbuf", [128, n], d)


SCRATCH = {
    "xt": sb(4 * C, BF), "ut": sb(512, BF), "vt": sb(512, BF),
    "pi": sb(K, I32), "qi": sb(K, I32), "mi": sb(K, I32),
    "wq": sb(512, MX), "wp": sb(512, U8), "uq": sb(128, MX), "up": sb(128, U8), "ur": sb(128, MX), "urp": sb(128, U8),
    "vq": sb(128, MX), "vp": sb(128, U8), "eq": sb(512, MX), "ep": sb(512, U8),
    "tq": sb(C, MX), "tp": sb(C, U8), "zq": sb(C, MX), "zp": sb(C, U8),
    "et": sb(2048, BF), "one": sb(512, BF), "zt": sb(4 * C, BF),
    "cc": sb(2 * C, BF), "tm": sb(C, F32), "dif": sb(C, F32), "ka": sb(C, F32), "kb": sb(C, F32),
    "hc": sb(C, F32), "hh": sb(2 * C, F16), "hm": sb(2 * C, F16), "ones": sb(2 * C, BF),
    "pp": sb(1, I32), "pm": sb(1, I32), "pf": sb(1, F32), "cor": sb(1, F32), "coj": sb(1, F32), "coh": sb(1, F32),
    "cw0": sb(K, F32), "cw": sb(K, F32), "ou0": sb(8, I32), "ou": sb(8, U16),
    "w0": sb(C, F32), "wm0": sb(C, F32), "cd": sb(C, F32),
    "pw": sb(K, U16), "qw": sb(K, U16), "low": sb(K, U16), "hiw": sb(K, U16), "dmw": sb(K, F32), "muf": sb(K, F32),
    "qa": sb(C, BF), "qb": sb(C, BF), "ex": sb(C, F32), "eh": sb(2 * C, F16),
    "wa": sb(C, F32), "wb": sb(C, F32), "wm": sb(C, F32),
    "dd": sb(C, F32), "ctr": sb(C, F32), "c5": sb(C, F32), "buf": sb(C + 8, F32), "bg": sb(C, F32), "lg": sb(C, BF),
    "vi": sb(K, I32), "lw": sb(K, U16), "tw": sb(K, I32), "t2": sb(K, F32), "ll": sb(K, F32),
    "ps2": sb(2 * K, F32), "pos": sb(2 * K, U16), "posr": sb(K, U16), "lin": sb(2 * C, BF), "linw": sb(2 * K, U16),
    "nf": sb(C, BF), "ss": sb(C, F32), "g2": sb(2 * C, BF), "fs": sb(2 * C, BF), "rs": sb(2 * C, BF), "ij": sb(2 * C, BF), "eij": sb(2 * C, F16),
    "cq": sb(K, F32), "lc": sb(2 * K, F32), "k3": sb(2 * K, F32), "de": sb(K, F32), "zl": sb(K, F32), "zm": sb(K, F32), "dp": sb(K, F32), "of": sb(K, F32), "ow": sb(K, U16),
    "mf": sb(C, BF), "mw": sb(K, U16),
    "st": sb(C, F32), "su": sb(C, F32), "sg": sb(C, BF),
    "sw": sb(K, U16), "sf": sb(C, BF), "yf": sb(C, BF), "yw": sb(K, U16),
    "hb": sb(4 * C, BF), "ga": sb(4 * C, BF), "rb": sb(4 * C, F32), "mb": sb(4 * C, F32), "yo": sb(C, F32),
    "ps": ("psum", [128, 4096], F32),
}
for _k in range(3):
    SCRATCH["rq%d" % _k] = sb(C, MX)
    SCRATCH["rp%d" % _k] = sb(C, U8)
for _k in range(7):
    SCRATCH["xf%d" % _k] = sb(C, BF)
    SCRATCH["xw%d" % _k] = sb(K, U16)
LOADS = ["pi", "qi", "mi", "xt", "ut", "vt", "wq", "wp"]
STORES = ["oy", "oq", "occ", "oss"]
SEMAPHORES = ["v", "s", "t", "g"] + ["ld_" + a for a in LOADS] + ["st_" + a for a in STORES] + ["arr%d" % k for k in range(3)] + ["snt%d" % k for k in range(3)]


def rank_program(g, core, T, topo):
    rank = T.rank_of(core)
    if rank is None:
        return
    queue = {"v": g.vector, "s": g.scalar, "t": g.tensor, "g": g, "y": g.sync}
    count, known, snap = {}, {e: {} for e in queue}, {}
    last, readers = {}, {}

    def settle(e, tokens):
        for s, n in sorted(tokens, key=lambda a: (a[0] == e, -a[1])):
            if known[e].get(s, 0) >= n: continue
            queue[e].wait_ge(T.sem[s], n)
            for a, b in list(snap.get((s, n), {}).items()) + [(s, n)]:
                known[e][a] = max(known[e].get(a, 0), b)

    def issue(n, e):
        tokens = set()
        for k in n["rd"]:
            if k in last: tokens.add(last[k])
        for k in n["wr"]:
            if k in last: tokens.add(last[k])
            tokens |= readers.get(k, set())
        settle(e, tokens)
        s = n["sem"] or e
        n["make"][e]().then_inc(T.sem[s], n["inc"])
        count[s] = count.get(s, 0) + n["inc"]
        token = (s, count[s])
        snap[token] = dict(known[e])
        snap[token][s] = count[s]
        for k in n["wr"]: last[k], readers[k] = token, set()
        for k in n["rd"]: readers.setdefault(k, set()).add(token)

    nodes = []

    def op(e, make, rd, wr, sem=None, inc=1, cost=TINY, lat=0.0, other=None, send=None):
        nodes.append(dict(make={e: make} if other is None else {e: make, other[0]: other[1]}, rd=rd, wr=wr, sem=sem, inc=inc, cost=cost, lat=lat, send=send))

    V, S = g.vector, g.scalar

    def ts(out, in0, s1, s2, o0, o1, rd, wr, cost=TINY):
        if o1 is None: op("v", lambda: V.tensor_scalar(out, in0, s1, None, o0), rd, wr, cost=cost)
        else: op("v", lambda: V.tensor_scalar(out, in0, s1, s2, o0, o1), rd, wr, cost=cost)

    def tt(out, a, b, o, rd, wr, cost=TINY):
        op("v", lambda: V.tensor_tensor(out, a, b, o), rd, wr, cost=cost)

    def cp(out, a, rd, wr, cost=TINY):
        op("v", lambda: V.tensor_copy(out, a), rd, wr, cost=cost)

    def either(out, a, rd, wr, cost=GATHER):
        op("s", lambda: S.activation(out, a, AF.Copy), rd, wr, cost=cost, other=("v", lambda: V.tensor_copy(out, a)))

    def act(out, a, f, rd, wr, bias=0.0, scale=1.0, cost=GATHER):
        if bias == 0.0 and scale == 1.0: op("s", lambda: S.activation(out, a, f), rd, wr, cost=cost)
        else: op("s", lambda: S.activation(out, a, f, bias=bias, scale=scale), rd, wr, cost=PLAIN)

    def scan(out, a, b, init, o0, o1, rd, wr, cost=PLAIN):
        op("v", lambda: V.tensor_tensor_scan(out, a, b, init, o0, o1), rd, wr, cost=cost)

    def load(e, name, out, in_):
        op(e, lambda: queue[e].dma_start(out, in_), [], [name], "ld_" + name, 16, cost=0.1, lat=2.5)

    def ordered():
        wrote, read, preds, succ = {}, {}, [], []
        for i, n in enumerate(nodes):
            p = set()
            for k in n["rd"]:
                if k in wrote: p.add(wrote[k])
            for k in n["wr"]:
                if k in wrote: p.add(wrote[k])
                p |= read.get(k, set())
            for k in n["wr"]: wrote[k], read[k] = i, set()
            for k in n["rd"]: read.setdefault(k, set()).add(i)
            p.discard(i)
            preds.append(p)
            succ.append([])
            for j in p: succ[j].append(i)
        rank_ = [0.0] * len(nodes)
        for i in range(len(nodes) - 1, -1, -1):
            rank_[i] = nodes[i]["cost"] + nodes[i]["lat"] + max([rank_[j] + WAKE for j in succ[i]] + [0.0])
        free, at, end, todo = {e: 0.0 for e in queue}, {}, {}, [len(p) for p in preds]
        open_, out = [i for i in range(len(nodes)) if not preds[i]], []
        while open_:
            best, spots = {}, {}
            waiting = min([max([end[j] + (NEAR if at[j] == "v" else WAKE) for j in preds[i]] + [0.0]) for i in open_ if list(nodes[i]["make"]) == ["v"]] + [1e9])
            for i in open_:
                spot = None
                for e in nodes[i]["make"]:
                    r = max([end[j] + (NEAR if at[j] == e else WAKE) for j in preds[i]] + [0.0])
                    t = max(r, free[e])
                    a = (t + (BIAS if e == "v" and len(nodes[i]["make"]) > 1 and waiting < t + GATHER * LOOK else 0.0), e, r)
                    if spot is None or a < spot: spot = a
                spots[i] = spot
                e, r = spot[1], max(spot[2], free[spot[1]])
                best[e] = min(best.get(e, 1e9), r)
            e = min(best, key=lambda a: (best[a], a))
            i = max([j for j in open_ if spots[j][1] == e and max(spots[j][2], free[e]) <= best[e] + SLACK], key=lambda j: (rank_[j], -j))
            t = max(spots[i][2], free[e])
            free[e], at[i], end[i] = t + nodes[i]["cost"], e, t + nodes[i]["cost"] + nodes[i]["lat"]
            open_.remove(i)
            out.append((nodes[i], e))
            for j in succ[i]:
                todo[j] -= 1
                if not todo[j]: open_.append(j)
        return out

    def held(name):
        scan(T.ex[:], T.hc[:], T[name][:], 0.0, O.add, O.max, ["hc", name], ["ex"])
        return T.ex[:, 15:C:16]

    def unwrap(name, n, w, more=[]):
        scan(T.eh[:, 0:n], T.hh[:, 0:n], T[name][:, 0:n], 0.0, O.add, O.max, ["hh", name] + more, ["eh"], HALF * n / C)
        ts(T[w][:, 0:n // 16], T.eh[:, 15:n:16], T.coh[:, 0:1], None, O.subtract, None, ["eh", "coh"], [w])

    def bank(b, n=C):
        return T.ps[:, 512 * b:512 * b + n]

    def mm(b, l, ls, a, r, rs, key=None):
        op("t", lambda: g.tensor.matmul_mx(bank(b), T[l][:, a:a + 128], T[ls][:, a:a + 128], T[r][:, 0:C], T[rs][:, 0:C], True, True),
           [r, rs] + ([key] if key else [l, ls]), ["ps%d" % b], cost=0.3)

    def quant(q, p, t, n, rd=None):
        op("v", lambda: V.quantize_mx(T[q][:, 0:n], T[p][:, 0:n], T[t][:, 0:4 * n]), rd or [t], [q, p], cost=0.32)

    def iota(name, out, pattern, base, mul, small=True):
        cost = 0.14 + 0.002 * (C if len(pattern) > 1 else pattern[0][1])
        if small: op("g", lambda: g.iota(out, pattern, base, mul, allow_small_or_imprecise_dtypes=True), [], [name], cost=cost)
        else: op("g", lambda: g.iota(out, pattern, base, mul), [], [name], cost=cost)

    load("y", "pi", T.pi[:], T.pl[:])
    load("s", "qi", T.qi[:], T.ql[:])
    load("y", "xt", T.xt[:], T.x[:])
    load("y", "ut", T.ut[:], T.u[:])
    load("y", "mi", T.mi[:], T.ml[:])
    load("y", "wq", T.wq[:].bitcast(dt.uint8), T.wc[:])
    load("y", "wp", T.wp[:], T.ws[:])
    load("y", "vt", T.vt[:], T.v[:])

    iota("pp", T.pp[:], [[1, 1]], 0, 1, False)
    iota("tm", T.tm[:], [[0, K], [1, 16]], 0, 0)
    iota("cc", T.cc[:, 0:C], [[1, C]], -MID, 0)
    iota("wm0", T.wm0[:], [[UNIT, C]], LIFT + SEEN - 1, 0)
    iota("w0", T.w0[:], [[UNIT, C]], LIFT + SEEN, 0)
    iota("ou0", T.ou0[:], [[16, 8]], 0, 0, False)
    iota("cw0", T.cw0[:], [[16, K]], 0, 0)
    op("v", lambda: V.memset(T.one[:], 1.0), [], ["one"])
    for b in range(4):
        op("g", lambda b=b: g.affine_select(T.et[:, 512 * b:512 * b + 512], T.one[:], [[-1, 512]], O.is_equal, 0.0, b, 4), ["one"], ["et%d" % b], cost=1.2)
    iota("cd", T.cd[:], [[UNIT, C]], LIFT - 1, 0)
    ts(T.pm[:], T.pp[:], 15, None, O.bitwise_and, None, ["pp"], ["pm"])
    cp(T.pf[:], T.pm[:], ["pm"], ["pf"])
    ts(T.cor[:], T.pf[:], 15.0, HOLD, O.is_lt, O.mult, ["pf"], ["cor"])
    ts(T.dif[:], T.tm[:], T.pf[:, 0:1], None, O.subtract, None, ["tm", "pf"], ["dif"])
    ts(T.ka[:], T.dif[:], 0.0, DROP, O.is_equal, O.mult, ["dif"], ["ka"])
    ts(T.kb[:], T.dif[:], 1.0, HOLD, O.is_equal, O.mult, ["dif"], ["kb"])
    tt(T.hc[:], T.ka[:], T.kb[:], O.add, ["ka", "kb"], ["hc"])
    ts(T.hh[:, 0:C], T.hc[:], 2.0 ** -10, None, O.mult, None, ["hc"], ["hh"])
    ts(T.coh[:], T.cor[:], 2.0 ** -10, float(MID), O.mult, O.subtract, ["cor"], ["coh"])

    cp(T.qw[:], T.qi[:], ["qi"], ["qw"])
    cp(T.pw[:], T.pi[:], ["pi"], ["pw"])
    act(T.qa[:], T.cc[:, 0:C].indirect(T.qw[:]), AF.Copy, ["cc", "qw"], ["qa"])
    act(T.xf0[:], T.qa[:].indirect(T.pw[:]), AF.Copy, ["qa", "pw"], ["xf0"])
    op("v", lambda: V.memset(T.ones[:], 1.0), [], ["ones"], cost=PLAIN)
    op("v", lambda: V.memset(T.buf[:, 0:8], 0.0), [], ["buf"])
    cp(T.cc[:, C:2 * C], T.cc[:, 0:C], ["cc"], ["cd2"], HALF)
    cp(T.hh[:, C:2 * C], T.hh[:, 0:C], ["hh"], ["hh2"], HALF)
    cp(T.ou[:], T.ou0[:], ["ou0"], ["ou"])

    def jump():
        unwrap("xf0", C, "xw0")
        w, wm, made = "w0", "wm0", 0
        for n, (k, s) in enumerate(JUMPS):
            if n:
                act(T.wm[:], T[w][:], AF.Identity, [w], ["wm"], bias=-float(s))
                wm = "wm"
            nxt = "wb" if w == "wa" else "wa"
            tt(T[nxt][:], T[w][:].indirect(T["xw%d" % k][:]), T[wm][:], O.min, [w, "xw%d" % k, wm], [nxt], GATHER)
            w = nxt
            if made == k and k < 6:
                either(T["xf%d" % (k + 1)][:], T["xf%d" % k][:].indirect(T["xw%d" % k][:]), ["xf%d" % k, "xw%d" % k], ["xf%d" % (k + 1)])
                unwrap("xf%d" % (k + 1), C, "xw%d" % (k + 1))
                made = k + 1
        tt(T.dd[:], T[w][:].indirect(T.xw0[:]), T.cd[:], O.subtract, [w, "xw0", "cd"], ["dd"], GATHER)
        for a, c in (("c5", 2.0), ("ctr", 1.0)):
            op("s", lambda a=a, c=c: S.activation(T[a][:], T.dd[:], AF.Relu, scale=c), ["dd"], [a], cost=PLAIN,
               other=("v", lambda a=a, c=c: V.tensor_scalar(T[a][:], T.dd[:], 0.0, c, O.max, O.mult)))
        a = held(w)
        ts(T.lw[:], a, T.cor[:, 0:1], 1.0 / UNIT, O.subtract, O.mult, ["ex", "cor"], ["lw"])
        ts(T.vi[:], a, T.cor[:, 0:1], float(LIFT), O.subtract, O.subtract, ["ex", "cor"], ["vi"])
        scan(T.buf[:, 1:C + 1], T.ones[:, 0:C], T.c5[:], 0.0, O.mult, O.add, ["ones", "c5"], ["buf"])
        either(T.bg[:], T.buf[:, 0:C].indirect(T.lw[:]), ["buf", "lw"], ["bg"])
        ts(T.tw[:], T.vi[:], UNIT - 1, None, O.bitwise_and, None, ["vi"], ["tw"])
        ts(T.t2[:], T.tw[:], T.cor[:, 0:1], None, O.subtract, None, ["tw", "cor"], ["t2"])
        either(T.lg[:], T.ctr[:].indirect(T.lw[:]), ["ctr", "lw"], ["lg"])
        scan(T.eh[:, 0:C], T.hh[:, 0:C], T.lg[:], 0.0, O.add, O.max, ["hh", "lg"], ["eh"], HALF)
        ts(T.ll[:], T.eh[:, 15:C:16], T.coh[:, 0:1], float(MID), O.subtract, O.subtract, ["eh", "coh"], ["ll"])
        a = held("bg")
        tt(T.ps2[:, 0:K], a, T.t2[:], O.add, ["ex", "t2"], ["psa"])
        tt(T.ps2[:, K:2 * K], T.ps2[:, 0:K], T.ll[:, 0:K], O.add, ["psa", "ll"], ["psb"])
        cp(T.pos[:], T.ps2[:], ["psa", "psb"], ["pos"])
        cp(T.lin[:].indirect(T.pos[:]), T.cc[:], ["pos", "cc", "cd2"], ["lin"], SCATTER)
        for a, w in ((0, "lca"), (K, "lcb")): ts(T.lc[:, a:a + K], T.ll[:], T.coj[:, 0:1], None, O.add, None, ["ll", "coj"], [w])
        ts(T.posr[:], T.ps2[:, 0:K], -1.0, float(2 * C - 1), O.mult, O.add, ["psa"], ["posr"])
        unwrap("lin", 2 * C, "linw", ["hh2"])

    def products():
        mm(4, "ur", "urp", 0, "tq", "tp")
        for b in range(4): mm(b, "eq", "ep", 128 * b, "tq", "tp", "eq%d" % b)

    def times(out, a, c, rd, wr):
        op("s", lambda: S.activation(out, a, AF.Identity, scale=c), rd, wr, cost=PLAIN, other=("v", lambda: V.tensor_scalar(out, a, c, None, O.mult)))

    def halves():
        for b in range(4): times(T.hb[:, C * b:C * b + C], bank(b), 0.5, [], ["ps%d" % b, "hb%d" % b])

    def aside():
        for b in range(4):
            either(T.ga[:, b:4 * C:4], T.hb[:, C * b:C * b + C].indirect(T.xw0[:]), ["hb%d" % b, "xw0"], ["ga%d" % b])

    def prepare():
        ts(T.hm[:], T.hh[:], 2.0, None, O.mult, None, ["hh", "hh2"], ["hm"], PLAIN)
        ts(T.coj[:], T.cor[:], 2.0 ** -9, None, O.mult, None, ["cor"], ["coj"])

    def prepare2():
        ts(T.cw[:], T.cw0[:], T.pf[:, 0:1], None, O.add, None, ["cw0", "pf"], ["cw"])
        tt(T.dmw[:], T.mi[:], T.cw[:], O.subtract, ["mi", "cw"], ["dmw"])
        ts(T.muf[:], T.dmw[:], T.cor[:, 0:1], 2.0 ** -10, O.mult, O.mult, ["dmw", "cor"], ["muf"])
        tt(T.cq[:], T.cw[:], T.muf[:], O.subtract, ["cw", "muf"], ["cq"])
        for w, o in (("low", O.min), ("hiw", O.max)):
            tt(T.muf[:], T.mi[:], T.cw[:], o, ["mi", "cw"], ["muf"])
            cp(T[w][:], T.muf[:], ["muf"], [w])

    def first():
        quant("uq", "up", "ut", 128)
        cp(T.ur[:].bitcast(dt.uint32), T.uq[:].bitcast(dt.uint32).indirect(T.ou[:]), ["uq", "ou"], ["ur"])
        cp(T.urp[:], T.up[:].indirect(T.ou[:]), ["up", "ou"], ["urp"])
        quant("tq", "tp", "xt", C)

    def constants():
        for b in range(4):
            op("v", lambda b=b: V.quantize_mx(T.eq[:, 128 * b:128 * b + 128], T.ep[:, 128 * b:128 * b + 128], T.et[:, 512 * b:512 * b + 512]), ["et%d" % b], ["eq%d" % b], cost=0.15)
        products()

    first()
    constants()
    prepare()
    prepare2()
    jump()
    quant("vq", "vp", "vt", 128)

    qcur = ["qa", "qb"]
    for k, step in enumerate(STEPS):
        final = k == 2
        peer = T.cores[rank ^ step]
        rid, pid = topo.addr(peer, core)
        mask = topo.mask(core, peer)
        width = len(topo.engines(core, peer))
        ts(T.nf[:], bank(4), 0.0, None, O.is_ge, None, [], ["ps4", "nf"], PLAIN)
        cp(T.g2[:, 0:16 * CUT], T.nf[:].indirect(T.linw[:, 0:CUT]), ["nf", "linw"], ["g2a"], GATHER * CUT / K)
        act(T.g2[:, 16 * CUT:2 * C], T.nf[:].indirect(T.linw[:, CUT:2 * K]), AF.Copy, ["nf", "linw"], ["g2b"], cost=GATHER * (2 * K - CUT) / K)
        act(T.ss[:], bank(4), AF.Copy, [], ["ps4", "ss"], cost=PLAIN)
        scan(T.fs[:], T.g2[:], T.ones[:], 1.0, O.mult, O.add, ["g2a", "g2b", "ones"], ["fs"])
        act(T.ij[:, 0:C], T.fs[:].indirect(T.pos[:, K:2 * K]), AF.Copy, ["fs", "pos"], ["ija"])
        scan(T.rs[:], T.g2[:, ::-1], T.ones[:], 1.0, O.mult, O.add, ["g2a", "g2b", "ones"], ["rs"])
        cp(T.ij[:, C:2 * C], T.rs[:].indirect(T.posr[:]), ["rs", "posr"], ["ijb"], GATHER)
        halves()
        aside()
        scan(T.eij[:], T.hm[:], T.ij[:], 0.0, O.add, O.max, ["hm", "ija", "ijb"], ["eij"])
        tt(T.k3[:], T.eij[:, 15:2 * C:16], T.lc[:], O.min, ["eij", "lca", "lcb"], ["k3"])
        tt(T.de[:], T.k3[:, K:2 * K], T.k3[:, 0:K], O.subtract, ["k3"], ["de"])
        ts(T.zl[:], T.de[:], 0.0, None, O.is_lt, None, ["de"], ["zl"])
        tt(T.dp[:], T.de[:], T.ps2[:, 0:K], O.add, ["de", "psa"], ["dp"])
        tt(T.zm[:], T.zl[:], T.ll[:, 0:K], O.mult, ["zl", "ll"], ["zm"])
        tt(T.of[:], T.zm[:], T.dp[:], O.add, ["zm", "dp"], ["of"])
        cp(T.ow[:], T.of[:], ["of"], ["ow"])
        either(T.mf[:], T.lin[:].indirect(T.ow[:]), ["lin", "ow"], ["mf"])
        unwrap("mf", C, "mw")
        act(T.st[:], T.ss[:].indirect(T.mw[:]), AF.Copy, ["ss", "mw"], ["st"])
        act(T.su[:], T.st[:].indirect(T.low[:]), AF.Copy, ["st", "low"], ["su"])
        parts = [(0, 8), (8, K)] if final else [(0, K)]
        for h, (a, z) in enumerate(parts):
            own = [h] if final else [0, 1]
            zs = ["zt%d%d" % (j, b) for b in range(4) for j in own]
            for b in range(4):
                tt(T.zt[:, 64 * a + b:64 * z:4], T.hb[:, C * b:C * b + C].indirect(T.mw[:, a:z]), T.ga[:, 64 * a + b:64 * z:4], O.add, ["hb%d" % b, "mw", "ga%d" % b], ["zt%d%d" % (j, b) for j in own], GATHER * (z - a) / K)
            op("v", lambda a=a, z=z: V.quantize_mx(T.zq[:, 16 * a:16 * z], T.zp[:, 16 * a:16 * z], T.zt[:, 64 * a:64 * z]), zs, ["zq0", "zq1"][h:], cost=0.32 * (z - a) / K)

            def send(k=k, pid=pid, rid=rid, mask=mask, a=16 * a, z=16 * z, h=h, n=2 * width * len(parts)):
                settle("g", {last["zq%d" % h]})
                land, sent = T.sem["arr%d" % k], T.sem["snt%d" % k]
                g.remote_dma(T["rq%d" % k][:, a:z].bitcast(dt.uint8), T.zq[:, a:z].bitcast(dt.uint8), land, sent, pid, rid, mask)
                g.remote_dma(T["rp%d" % k][:, a:z], T.zp[:, a:z], land, sent, pid, rid, mask)
                readers.setdefault("zq%d" % h, set()).add(("snt%d" % k, n))
                for r in ("rq%d" % k, "rp%d" % k): last[r] = ("arr%d" % k, n)
                count["arr%d" % k] = count["snt%d" % k] = n

            op("g", None, ["zq%d" % h], ["rq%d" % k, "rp%d" % k], cost=0.6, lat=FLIGHT, send=send)
        tt(T.sg[:], T.st[:].indirect(T.hiw[:]), T.su[:], O.is_lt, ["st", "hiw", "su"], ["sg"], GATHER)
        scan(T.eh[:, 0:C], T.hh[:, 0:C], T.sg[:], 0.0, O.add, O.max, ["hh", "sg"], ["eh"], HALF)
        tt(T.zm[:], T.eh[:, 15:C:16], T.dmw[:], O.mult, ["eh", "dmw"], ["zm"])
        tt(T.of[:], T.zm[:], T.cq[:], O.add, ["zm", "cq"], ["of"])
        cp(T.sw[:], T.of[:], ["of"], ["sw"])
        qo, qn = qcur[k % 2], qcur[1 - k % 2]
        either(T.yf[:], T[qo][:].indirect(T.sw[:]), [qo, "sw"], ["yf"])
        either(T.sf[:], T.cc[:, 0:C].indirect(T.sw[:]), ["cc", "sw"], ["sf"])
        unwrap("yf", C, "yw")
        either(T[qn][:], T.sf[:].indirect(T.yw[:]), ["sf", "yw"], [qn])
        if not final:
            either(T.xf0[:], T[qn][:].indirect(T.pw[:]), [qn, "pw"], ["xf0"])
        else:
            ts(T.dd[:], T[qn][:], float(MID), None, O.add, None, [qn], ["dd"], PLAIN)
            op("y", lambda: g.sync.dma_start(T.qo[:], T.dd[0:128:16, :]), ["dd"], [], "st_oq", 16, lat=2.5)

        def layer():
            for b in range(4): mm((5, 6, 7, 4)[b], "wq", "wp", 128 * b, "rq%d" % k, "rp%d" % k)

        def scaled(bs):
            for b in bs:
                times(T.rb[:, C * b:C * b + C], bank((5, 6, 7, 4)[b]), 0.03125, [], ["ps%d" % (5, 6, 7, 4)[b], "rb%d" % b])

        def picked(bs):
            for b in bs:
                either(T.mb[:, C * b:C * b + C], T.rb[:, C * b:C * b + C].indirect(T.mw[:]), ["rb%d" % b, "mw"], ["mb%d" % b])

        def added(bs=range(4)):
            for b in bs:
                tt(T.xt[:, b:4 * C:4], T.mb[:, C * b:C * b + C], bank(b), O.add, ["mb%d" % b], ["ps%d" % b, "xt%d" % b], PLAIN)
            quant("tq", "tp", "xt", C, ["xt", "xt0", "xt1", "xt2", "xt3"])

        if not final:
            layer()
            scaled(range(4))
            picked(range(4))
            added()
            products()
            jump()
        else:
            layer()
            for b in (0, 1):
                cp(T.mb[:, C * b:C * b + C], bank(b), [], ["ps%d" % b, "mb%d" % b], PLAIN)
            scaled(range(4))
            picked([2, 3])
            for b in (0, 1):
                tt(T.xt[:, b:4 * C:4], T.rb[:, C * b:C * b + C].indirect(T.mw[:]), T.mb[:, C * b:C * b + C], O.add, ["rb%d" % b, "mw", "mb%d" % b], ["xt%d" % b], GATHER)
            added([2, 3])
            op("y", lambda: g.sync.dma_start(T.oc[:], T.tq[:].bitcast(dt.uint8)), ["tq"], [], "st_occ", 16, lat=2.5)
            for a in range(4):
                op("y", lambda a=a: g.sync.dma_start(T.osc[4 * a:4 * a + 4, :], T.tp[32 * a:32 * a + 4, :]), ["tp"], [], "st_oss", 16, lat=2.5)
            mm(4, "vq", "vp", 0, "tq", "tp")
            act(T.yo[:], bank(4), AF.Copy, [], ["ps4", "yo"], cost=PLAIN)
            op("y", lambda: g.sync.dma_start(T.y[:], T.yo[:]), ["yo"], [], "st_oy", 16, lat=2.5)
    for n, e in ordered():
        if n["send"]: n["send"]()
        else: issue(n, e)
    settle("g", set(count.items()))
